import numpy as np, ml_dtypes
CORES = [51,54,179,182]
N = 4
BF = ml_dtypes.bfloat16
P, BK, W, SH, NB, EV = 256, 4096, 16, 4, 2048, 5
LV, AR, LIVE = 32, 48, 448
def group():
    return np.arange(8)[None, :, None]
def event(bm, cs, ls, e, sd, t):
    q = e >> 16; u = e & 65535; g = group()
    m = bm[q, g, u >> SH]; b = (m >> 5) + ((u & (W - 1)) >= (m & 31))
    c = cs.reshape(N, 8, 16, NB)[q, g, :, b]
    k = np.sum(c <= ((sd >> (4 * t)) & 4095)[..., None], axis=-1)
    return c, np.maximum(e - ls.reshape(N, 8, 16, NB)[q, g, k, b].astype(np.float32).astype(np.int64), 0)
def first(rng, key, on, cap):
    k = np.where(on, key, 9999); o = np.lexsort((rng.random(k.size), k)); s = k[o]; r = np.empty_like(o)
    r[o] = np.arange(s.size) - np.searchsorted(s, s); return on & (r < cap)
def plant(rng, d, u, sd):
    e = u + 65536 * np.arange(N)[:, None, None]; d["en"] = e.astype(np.int32); g = np.broadcast_to(group(), e.shape).ravel()
    for t in range(EV - 1):
        s = sd + (rng.integers(0, 16, sd.shape) << (8 + 4 * t)); v = event(d["bm"], d["cs"], d["ls"], e, s, t)[1]
        a = (e >> 16).ravel(); z = (v >> 16).ravel()
        ok = first(rng, z * 8 + g, first(rng, (a * N + z) * 8 + g, a != z, LV), AR)
        no = ((a != z) & ~ok).reshape(e.shape); sd = np.where(no, sd, s); e = np.where(no, e, v)
    d["sd"] = sd.astype(np.int32); return d
def sections(c):
    return c.reshape(N, 128, NB).astype(np.int32)
def losses(v):
    v[:, :, 0] = 0; return v.reshape(N, 128, NB).astype(np.float32).astype(BF)
def setup_inputs(rng):
    h = np.zeros((N, 8, BK), np.int64); h[:, :, -1] = 1
    np.put_along_axis(h[..., :-1], np.argsort(rng.random((N, 8, BK - 1)), axis=-1)[..., :NB - 2], 1, -1)
    bm = (np.cumsum(h, axis=-1) - h) * 32 + np.where(h == 1, rng.integers(0, W, h.shape), W)
    c = np.sort(rng.integers(256, 4097, (N, 8, 16, NB)), axis=2); c[:, :, 15] = rng.integers(4096, 8192, (N, 8, NB))
    v = rng.integers(0, 256, c.shape) << rng.integers(0, 10 + 1, c.shape)
    d = {"bm": bm.astype(np.int32), "cs": sections(c), "ls": losses(v), "en": None, "sd": None}
    return plant(rng, d, rng.integers(0, 65536, (N, 8, P)), rng.integers(0, 256, (N, 8, P)))
def setup_inputs_full(rng):
    d = setup_inputs(rng); v = losses(rng.integers(64, 256, (N, 8, 16, NB)) * 512); d["ls"][1:] = v[1:]
    return plant(rng, d, rng.integers(0, 65536, (N, 8, P)), rng.integers(0, 256, (N, 8, P)))
def setup_inputs_ends(rng):
    d = setup_inputs(rng); m = d["bm"]; n = (N, 8, P)
    d["bm"] = np.where((m & 31) < W, (m >> 5) * 32 + rng.choice(np.array([0, 1, W - 1]), m.shape), m).astype(np.int32)
    c = 256 * np.sort(rng.integers(1, 17, (N, 8, 16, NB)), axis=2); c[:, :, 15] = rng.choice(np.array([4096, 8191]), (N, 8, NB)); d["cs"] = sections(c)
    d["ls"] = losses(rng.choice(np.array([0, 1, 1, 2, 255, 32768, 65280, 65536, 131072, 65536 * N]), c.shape))
    u = W * rng.integers(0, BK, n) + rng.choice(np.array([0, 1, W - 1]), n)
    u = np.where(rng.random(n) < 0.25, rng.choice(np.array([0, 1, 65534, 65535]), n), u)
    return plant(rng, d, u, np.zeros(n, np.int64))
def setup_inputs_still(rng):
    d = setup_inputs(rng); w = (N, 8, 16, NB)
    c = np.sort(rng.integers(0, 4097, w), axis=2); c[:, :, 15] = rng.integers(4096, 8192, (N, 8, NB)); d["cs"] = sections(c)
    d["ls"] = rng.integers(1, 256, w).reshape(N, 128, NB).astype(np.float32).astype(BF)
    return plant(rng, d, rng.integers(4096, 65536, (N, 8, P)), rng.integers(0, 256, (N, 8, P)))
def setup_inputs_spread(rng):
    d = setup_inputs(rng); w = (N, 8, 16, NB)
    d["bm"] = ((rng.random((N, 8, BK)) ** 4 * (NB - 1)).astype(np.int64) * 32 + rng.integers(0, W + 1, (N, 8, BK))).astype(np.int32)
    c = 256 + (rng.random(w) ** 3 * 7936).astype(np.int64); c[:, :, 15] = np.maximum(c[:, :, 15], 4096); d["cs"] = sections(c)
    d["ls"] = losses((rng.random(w) ** 4 * 256).astype(np.int64) << rng.integers(0, 10 + 1, w))
    return plant(rng, d, (rng.random((N, 8, P)) ** 4 * 65536).astype(np.int64), rng.integers(0, 256, (N, 8, P)))
def check_inputs(d):
    bad = []; m = d["bm"]; c = d["cs"].reshape(N, 8, 16, NB); v = d["ls"].astype(np.float32); e = d["en"].astype(np.int64); s = d["sd"].astype(np.int64)
    if not ((m >= 0) & ((m >> 5) <= NB - 2) & ((m & 31) <= W)).all(): bad.append("buckets")
    if not ((c >= 0) & (c <= 8191)).all() or not (c[:, :, 15] >= 4096).all(): bad.append("sections")
    if not ((v >= 0) & (v <= 65536 * N) & (v == np.floor(v))).all(): bad.append("losses")
    if not ((e >> 16) == np.arange(N)[:, None, None]).all(): bad.append("energies")
    if not ((s >= 0) & (s < 16 ** (EV + 1))).all(): bad.append("seeds")
    if bad: return bad
    for t in range(EV - 1):
        a = e >> 16; e = event(m, d["cs"], d["ls"], e, s, t)[1]; z = e >> 16
        n = np.bincount(((a * N + z) * 8 + group()).ravel(), minlength=N * N * 8).reshape(N, N, 8)
        if (n[~np.eye(N, dtype=bool)] > LV).any(): bad.append("leavers")
        if (np.sum(n, axis=0) > LIVE).any(): bad.append("live")
    return sorted(set(bad))
def reference(bm, cs, ls, en, sd):
    e = en.astype(np.int64); s = sd.astype(np.int64); tally = np.zeros((N, 8, P, 16), np.int64)
    for t in range(EV):
        c, e = event(bm, cs, ls, e, s, t)
        tally += c
    return {"y": tally.transpose(0, 1, 3, 2).reshape(N, 128, P).astype(np.float32)}

@@ -1,0 +1,490 @@
+from concourse.bass import DstId, RemoteDMATransfer
+from concourse.mybir import AluOpType as A, ActivationFunctionType as AF
+
+NR, P, W = 4, 256, 16
+BIG, LOW, MID = float(1 << 22), float(1 << 19), 2048.0
+CFG = {
+    "bm": (0, 0, 0, 0), "cs": (1, 0, 0, 0), "ls": (0, 1, 1, 1), "mask": (1, 0, 0, 0),
+    "streams": (((0, 1), (1, 2), (2, 3), (3, 4)), ((1, 2), (2, 3), (3, 4)), ((2, 3), (3, 4)), ((3, 4),)),
+    "cyc": 1.04, "gat": 1.56, "hop": 110.0, "pe": 0.52, "rem": 2500.0, "t_cs": 6500.0, "t_ls": 8500.0,
+    "look": 100.0, "lk2": 0.5, "marg": 1000.0, "seed": 1, "noise": 0.0, "tw": 256,
+    "prio": {"210": -300, "021": -1500, "121": 1500, "240": -1500, "011": -3000, "120": -1500, "040": 300, "140": -1200,
+             "142": -1100, "221": -1500, "042": 1000, "041": -3000, "131": 300, "241": -3000, "031": -700, "230": 1500,
+             "043": -3000, "130": 2700, "122": -700, "020": -1500, "152": -1500, "032": 3000, "000": 700, "010": 700},
+}
+
+F, I, H, B, U = "float32", "int32", "float16", "bfloat16", "uint16"
+SCRATCH = {k: ("sbuf", [128, n], t) for k, n, t in (
+    ("bmc", 512, I), ("bmt", 512, I), ("cc", 256, F), ("hl", 512, H), ("yt", 4112, F), ("csi", 2056, I), ("csf", 2056, F),
+    ("lsb", 2064, B), ("ia", 128, I), ("ib", 128, I), ("ibh", 128, H), ("sm", 1024, H), ("ones", 128, F), ("f0", 128, F),
+    ("f1", 128, F), ("fb", 128, B), ("hm", 144, B), ("zb", 512, B), ("idn", 128, F), ("g8", 128, F), ("g8h", 128, H),
+    ("i16", 32, I), ("j16", 32, I), ("col", 32, F), ("wm", 512, F), ("d0", 1024, F), ("sdi", 16, I), ("vi", 64, I),
+    ("vf", 64, H), ("vl", 192, H), ("vc", 3328, H), ("vb", 3328, F), ("eni", 32, I), ("enf", 32, F), ("ent", 32, F),
+    ("enm", 32, F), ("es", 384, F), ("land", 256, F), ("o1", 384, U), ("o2", 384, U), ("xx", 1024, F), ("yy", 1024, F),
+    ("cg", 2048, F), ("ab", 1024, F), ("lg", 1024, B), ("cmpb", 1024, B), ("msk", 1024, B), ("selb", 1024, B),
+    ("tl", 1024, F), ("tu", 2048, U), ("tin", 1536, U), ("acc", 2048, F))}
+for _b in range(8):
+    SCRATCH["pb%d" % _b] = ("psum", [128, 512], F)
+
+SEMAPHORES = (["nv", "na", "nt", "ng", "sent"] + ["d%d" % i for i in range(14)] + ["v%d" % h for h in range(NR)]
+              + ["r%d%d%d" % (s, k, t) for s in range(1, NR) for k in range(3) for t in range(4)]
+              + ["f%d%d" % (s, k) for s in range(NR) for k in range(2)])
+COUNT = {"v": "nv", "a": "na", "p": "nt", "g": "ng"}
+
+
+def tasks_of(q, streams):
+    out = [(0, 0, q, q + 1, q), (1, 0, q, q + 1, q)]
+    for r in range(2, 6):
+        for st in range(len(streams) - 1, -1, -1):
+            a, b = streams[st]
+            if r == 5:
+                a = max(a, q + 1)
+                if a < b:
+                    out.append((r, st, a, b, b))
+            else:
+                out.append((r, st, a, b, max(a, q + 1) if r == 4 else a))
+    return out
+
+
+def event_of(q, h, r):
+    return r if h == q else r - 1
+
+
+def build(cores, topo, cfg):
+    ops, hist = [], {}
+    CYC, GAT, HOP = cfg["cyc"], cfg["gat"], cfg["hop"]
+    TASKS = [tasks_of(q, cfg["streams"][q]) for q in range(NR)]
+    closing, tag = {}, [None]
+
+    def add(q, eng, fn, busy, rd=(), wr=(), lat=0.0, sem=None, remote=None):
+        i = len(ops)
+        deps = set()
+        for acc, write in ((rd, False), (wr, True)):
+            for a in acc:
+                r, name, lo, hi = a if len(a) == 4 else (q,) + tuple(a)
+                for (j, e2, l2, h2, w2) in hist.setdefault((r, name), []):
+                    if j == i:
+                        continue
+                    meet = lo < h2 and l2 < hi and (write or w2)
+                    if meet or (name.startswith("pb") and e2 != eng):
+                        deps.add(j)
+                hist[(r, name)].append((i, eng, lo, hi, write))
+        ops.append({"q": q, "e": eng, "fn": fn, "busy": busy, "lat": lat, "deps": deps, "sem": sem, "rem": remote,
+                    "w": list(wr)[0], "tag": tag[0]})
+        return i
+
+    def vec(q, fn, cyc, rd, wr):
+        return add(q, "v", fn, 45 + max(64, cyc) * CYC, rd, wr)
+
+    def act(q, fn, cyc, rd, wr):
+        return add(q, "a", fn, 60 + max(64, cyc) * CYC, rd, wr)
+
+    def pe(q, fn, cyc, rd, wr):
+        return add(q, "p", fn, 30 + cyc * cfg["pe"], rd, wr)
+
+    def gp(q, fn, n, rd, wr):
+        return add(q, "g", fn, 150 + 2 * n * CYC, rd, list(wr) + [("order", 0, 1)])
+
+    def fill(q, name, sl, n, c, reg, rows=slice(0, 128)):
+        return act(q, lambda g, T: g.scalar.activation(T[name][rows, sl], T.ones[rows, 0:n], AF.Copy, scale=c), n, [("ones", 0, 128)], [reg])
+
+    ndma = [0] * NR
+
+    def dma(q, eng, fn, lat, rd, wr):
+        ndma[q] += 1
+        i = add(q, eng, fn, 80, rd, wr, lat=lat, sem=("d%d" % (ndma[q] - 1), 16))
+        ops[i]["boost"] = 1e6 - 1e4 * ndma[q]
+        return i
+
+    def split_engines(q, dsts, leave):
+        can = {d: topo.engines(cores[q], cores[d]) for d in list(dsts) + list(leave)}
+        least = min(len(v) for v in can.values())
+        used, res = set(), {}
+        for d in leave:
+            used.update(can[d])
+        for part in ([d for d in dsts if len(can[d]) == least], [d for d in dsts if len(can[d]) > least]):
+            if part:
+                free = [e for e in can[part[0]] if e not in used and all(e in can[d] for d in part)]
+                n = 1
+                while 2 * n * len(part) <= len(free):
+                    n *= 2
+                for x, d in enumerate(part):
+                    res[d] = free[x * n:(x + 1) * n]
+                    used.update(res[d])
+        return res
+
+    def send(q, sem, items, lat, leave=()):
+        eng = split_engines(q, [it[0] for it in items], leave)
+
+        def fn(g, T):
+            tr = []
+            for (d, sb, lo, hi, db, dlo) in items:
+                rid, pid = topo.addr(cores[d], cores[q])
+                tr.append(RemoteDMATransfer(dst_ids=[DstId(rid=rid, pnc=pid)], dma_engine_mask=sum(1 << e for e in eng[d]),
+                                            remote_sem=T.sem[sem], src=T[sb][:, lo:hi], dst=T[db][:, dlo:dlo + hi - lo]))
+            g.remote_dma_fused(tr, local_sem=T.sem.sent)
+            return None
+        return add(q, "g", fn, 500, [(it[1], it[2], it[3]) for it in items],
+                   [(it[0], it[4], it[5], it[5] + it[3] - it[2]) for it in items], lat=lat,
+                   remote=(sem, {d: len(e) for d, e in eng.items()}))
+
+    vpos = {}
+    for q in range(NR):
+        n = 0
+        for (r, _, h0, h1, h2) in TASKS[q]:
+            for h in range(h2, h1):
+                vpos[(q, h, event_of(q, h, r))] = n
+                n += P
+
+    def vbanks(q):
+        return ["pb%d" % b for b in range(3 + len(cfg["streams"][q]), 8)] + ["pb2"]
+
+    def start(q):
+        wide = P * max(b - a for a, b in cfg["streams"][q])
+        one = [("ones", 0, 128)]
+        dma(q, "s", lambda g, T: g.sync.dma_start(T.bmc[0:64, :], T.bm[:]), 2000, [], [("bmc0", 0, 1)])
+        dma(q, "a", lambda g, T: g.scalar.dma_start(T.bmc[64:128, :], T.bm[:]), 2000, [], [("bmc1", 0, 1)])
+        dma(q, "a", lambda g, T: g.scalar.dma_start(T.sdi[:], T.sd[:]), 2000, [], [("sdi", 0, 16)])
+        dma(q, "s", lambda g, T: g.sync.dma_start(T.eni[:, 0:16], T.en[:]), 2100, [], [("eni", 0, 16)])
+        dma(q, "a", lambda g, T: g.scalar.dma_start(T.eni[:, 16:32], T.en[:]), 2100, [], [("eni", 16, 32)])
+        dma(q, "s", lambda g, T: g.sync.dma_start(T.csi[:, 8:2056], T.cs[:]), cfg["t_cs"], [], [("csi", 8, 2056)])
+        dma(q, "s", lambda g, T: g.sync.dma_start(T.lsb[:, 8:2056], T.ls[:]), cfg["t_ls"], [], [("lsb", 8, 2056)])
+        vec(q, lambda g, T: g.vector.memset(T.ones[:], 1.0), 128, [], one)
+        gp(q, lambda g, T: g.iota(T.ia[:], [[-8, 8], [0, 16]], 64, 1), 128, [], [("ia", 0, 128)])
+        gp(q, lambda g, T: g.iota(T.i16[:, 0:17], [[-1, 17]], 16, 1), 17, [], [("i16", 0, 17)])
+        gp(q, lambda g, T: g.iota(T.cc[:], [[-1, 256]], 0, 0, allow_small_or_imprecise_dtypes=True), 256, [], [("cc", 0, 256)])
+        gp(q, lambda g, T: g.affine_select(T.g8[0:8, :], T.ones[0:8, :], [[-1, 8], [0, 16]], A.is_equal, 0.0, 0, 1), 128, one, [("g8", 0, 128)])
+        gp(q, lambda g, T: g.affine_select(T.f0[:], T.ones[:], [[-16, 8], [0, 16]], A.is_ge, 0.0, 0, 1), 128, one, [("f0", 0, 128)])
+        gp(q, lambda g, T: g.affine_select(T.f1[:], T.f0[:], [[16, 8], [0, 16]], A.is_ge, 0.0, 15, -1), 128, [("f0", 0, 128)], [("f1", 0, 128)])
+        gp(q, lambda g, T: g.affine_select(T.idn[:], T.ones[:], [[-1, 128]], A.is_equal, 0.0, 0, 1), 128, one, [("idn", 0, 128)])
+        vec(q, lambda g, T: g.vector.tensor_copy(T.g8h[0:8, :], T.g8[0:8, :]), 128, [("g8", 0, 128)], [("g8h", 0, 128)])
+        fill(q, "col", slice(0, 1), 1, 32.0, ("colA", 0, 1), slice(0, 64))
+        fill(q, "col", slice(0, 1), 1, -1.0, ("colB", 0, 1), slice(64, 128))
+        vec(q, lambda g, T: g.vector.tensor_scalar(T.ib[:], T.ia[:], 63, None, A.bitwise_and), 128, [("ia", 0, 128)], [("ib", 0, 128)])
+        vec(q, lambda g, T: g.vector.tensor_copy(T.ibh[:], T.ib[:]), 128, [("ib", 0, 128)], [("ibh", 0, 128)])
+        for o in range(8):
+            vec(q, lambda g, T, o=o: g.vector.tensor_scalar(T.sm[:, 128 * o:128 * o + 128], T.ibh[:], float(o), T.col[:, 0:1], A.is_equal, A.mult),
+                64, [("ibh", 0, 128), ("colA", 0, 1), ("colB", 0, 1)], [("sm", 128 * o, 128 * o + 128)])
+        act(q, lambda g, T: g.scalar.activation(T.fb[:], T.f1[:], AF.Copy), 128, [("f1", 0, 128)], [("fb", 0, 128)])
+        fill(q, "hm", slice(0, 128), 128, 0.0, ("hm", 0, 128))
+        fill(q, "hm", slice(128, 144), 16, 0.0, ("hm", 128, 144))
+        act(q, lambda g, T: g.scalar.activation(T.hm[:, 16:144:16], T.f1[:, 0:128:16], AF.Copy, scale=-1.0), 8, [("f1", 0, 128)], [("hm", 0, 144)])
+        vec(q, lambda g, T: g.vector.tensor_scalar(T.j16[:, 0:16], T.i16[:, 0:16], 15, None, A.bitwise_and), 16, [("i16", 0, 17)], [("j16", 0, 16)])
+        vec(q, lambda g, T: g.vector.tensor_scalar(T.j16[:, 16:17], T.i16[:, 16:17], 4, 1, A.logical_shift_right, A.bitwise_and), 1, [("i16", 0, 17)], [("j16", 16, 17)])
+        vec(q, lambda g, T: g.vector.tensor_scalar(T.wm[:, 0:16], T.j16[:, 0:16], 0.0, None, A.is_equal), 16, [("j16", 0, 16)], [("wm", 0, 16)])
+        sg = -1.0 if cfg["mask"][q] else 1.0
+        vec(q, lambda g, T: g.vector.tensor_scalar(T.col[:, 4:5], T.j16[:, 0:1], sg, None, A.mult), 1, [("j16", 0, 16)], [("col", 4, 5)])
+        vec(q, lambda g, T: g.vector.tensor_copy(T.col[:, 8:9], T.j16[:, 16:17]), 1, [("j16", 16, 17)], [("col", 8, 9)])
+        act(q, lambda g, T: g.scalar.activation(T.col[:, 12:13], T.col[:, 8:9], AF.Identity, bias=1.0, scale=-1.0), 1, [("col", 8, 9)], [("col", 12, 13)])
+        n = 16
+        while n < wide:
+            act(q, lambda g, T, n=n: g.scalar.activation(T.wm[:, n:2 * n], T.wm[:, 0:n], AF.Copy), n, [("wm", 0, n)], [("wm", n, 2 * n)])
+            n *= 2
+        for x in range(P * q, P * NR, 128):
+            fill(q, "d0", slice(x, x + 128), 128, -BIG, ("d0", x, x + 128))
+        if q > 0:
+            fill(q, "yt", slice(0, 8), 8, -BIG, ("yt", 0, 8))
+        fill(q, "yt", slice(4104, 4112), 8, -BIG, ("yt", 4104, 4112))
+        vec(q, lambda g, T: g.vector.memset(T.csi[:, 0:8], 0), 8, [], [("csi", 0, 8)])
+        fill(q, "lsb", slice(0, 8), 8, 0.0, ("lsb", 0, 8))
+        for t in range(4):
+            vec(q, lambda g, T, t=t: g.vector.tensor_scalar(T.vi[:, 16 * t:16 * t + 16], T.sdi[:], 4 * t, 4095, A.logical_shift_right, A.bitwise_and),
+                16, [("sdi", 0, 16)], [("vi", 16 * t, 16 * t + 16)])
+        vec(q, lambda g, T: g.vector.tensor_scalar(T.vf[:], T.vi[:], -MID, None, A.add), 64, [("vi", 0, 64)], [("vf", 0, 64)])
+        for t in range(4):
+            x = vpos[(q, q, t)]
+            add(q, "s", lambda g, T, t=t, x=x: g.sync.dma_start(T.vc[0:8, x:x + P], T.vf[:, 16 * t:16 * t + 16]), 80,
+                [("vf", 0, 64)], [("vc", x, x + P)], lat=2200, sem=("d13" if t else "d12", 48 if t else 16))
+        if q > 0:
+            send(q, "v%d" % q, [(d, "vf", 16, 64, "vl", 48 * q) for d in range(q - 1, -1, -1)], cfg["rem"] + 1500)
+        vec(q, lambda g, T: g.vector.tensor_copy(T.enf[:], T.eni[:]), 32, [("eni", 0, 32)], [("enf", 0, 32)])
+        vec(q, lambda g, T: g.vector.transpose(T.ent[:], T.enf[:]), 32, [("enf", 0, 32)], [("ent", 0, 32)])
+        act(q, lambda g, T: g.scalar.activation(T.enm[:, 0:16], T.ent[:, 0:16], AF.Identity, scale=T.col[:, 12:13]), 16, [("ent", 0, 32), ("col", 12, 13)], [("enm", 0, 16)])
+        act(q, lambda g, T: g.scalar.activation(T.enm[:, 16:32], T.ent[:, 16:32], AF.Identity, scale=T.col[:, 8:9]), 16, [("ent", 0, 32), ("col", 8, 9)], [("enm", 16, 32)])
+        vec(q, lambda g, T: g.vector.tensor_tensor(T.es[:, W * q:W * q + W], T.enm[:, 0:16], T.enm[:, 16:32], A.add), 32, [("enm", 0, 32)], [("es", W * q, W * q + W)])
+        vec(q, lambda g, T: g.vector.tensor_scalar(T.bmt[0:64, :], T.bmc[0:64, :], 5, None, A.logical_shift_right), 512, [("bmc0", 0, 1)], [("bmt0", 0, 1)])
+        vec(q, lambda g, T: g.vector.tensor_scalar(T.bmt[64:128, :], T.bmc[64:128, :], 31, None, A.bitwise_and), 512, [("bmc1", 0, 1)], [("bmt1", 0, 1)])
+        half = [("colC", 0, 1), ("colD", 0, 1)]
+        fill(q, "col", slice(16, 17), 1, 1.0, half[0], slice(0, 64))
+        fill(q, "col", slice(16, 17), 1, 0.0, half[1], slice(64, 128))
+        act(q, lambda g, T: g.scalar.activation(T.col[:, 20:21], T.col[:, 16:17], AF.Identity, bias=16.0, scale=-16.0), 1, half, [("col", 20, 21)])
+        act(q, lambda g, T: g.scalar.activation(T.pb7[:, 0:512:2], T.cc[:], AF.Identity, scale=T.col[:, 16:17]), 256, half + [("cc", 0, 256)], [("pb7", 0, 1)])
+        act(q, lambda g, T: g.scalar.activation(T.pb7[:, 1:512:2], T.cc[:], AF.Identity, bias=T.col[:, 20:21], scale=T.col[:, 16:17]), 256,
+            half + [("cc", 0, 256), ("col", 20, 21)], [("pb7", 1, 2)])
+        vec(q, lambda g, T: g.vector.tensor_tensor(T.hl[:], T.bmt[:], T.pb7[:], A.add), 512,
+            [("bmt0", 0, 1), ("bmt1", 0, 1), ("pb7", 0, 512)], [("hl", 0, 512)])
+        for o in range(8):
+            b = "pb%d" % (3 + o % 4)
+            lo = 8 + 512 * o
+            c = 16.5 - 8192.0 * o - 65536.0 * q - LOW
+            pe(q, lambda g, T, o=o, b=b: g.tensor.matmul(T[b][:], T.sm[:, 128 * o:128 * o + 128], T.hl[:], True, True), 512,
+               [("sm", 128 * o, 128 * o + 128), ("hl", 0, 512)], [(b, 0, 512)])
+            if o % 2 == 0:
+                act(q, lambda g, T, b=b, lo=lo, c=c: g.scalar.activation(T.yt[:, lo:lo + 512], T[b][:], AF.Identity, bias=c), 512, [(b, 0, 512)], [("yt", lo, lo + 512)])
+            else:
+                vec(q, lambda g, T, b=b, lo=lo, c=c: g.vector.tensor_scalar(T.yt[:, lo:lo + 512], T[b][:], c, None, A.add), 512, [(b, 0, 512)], [("yt", lo, lo + 512)])
+        if cfg["cs"][q]:
+            for x in range(0, 512, 128):
+                fill(q, "zb", slice(x, x + 128), 128, 0.0, ("zb", x, x + 128))
+            for b in ("pb0", "pb1"):
+                if b == "pb0" or q < NR - 1:
+                    pe(q, lambda g, T, b=b: g.tensor.matmul(T[b][:], T.zb[:, 0:128], T.zb[:], True, False), 512, [("zb", 0, 512)], [(b, 0, 512)])
+            for x in range(0, 2048, 512):
+                hi = x + 512 + (8 if x == 1536 else 0)
+                vec(q, lambda g, T, x=x, hi=hi: g.vector.tensor_scalar(T.csf[:, x:hi], T.csi[:, x:hi], -MID, None, A.add), 512, [("csi", x, hi)], [("csf", x, hi)])
+
+    def visitors_v(q):
+        for k, h in enumerate(range(q + 1, NR)):
+            for t in range(1, 4):
+                x = vpos[(q, h, t)]
+                add(q, "s", lambda g, T, h=h, t=t, x=x: g.sync.dma_start(T.vc[0:8, x:x + P], T.vl[:, 48 * h + 16 * t - 16:48 * h + 16 * t]), 80,
+                    [("vl", 48 * h, 48 * h + 48)], [("vc", x, x + P)], lat=2300, sem=("d%d" % (9 + k), 48))
+
+    def tally_at(q, h):
+        if not cfg["cs"][q]:
+            return "tl", P * h
+        if q == 0:
+            return "pb%d" % (h // 2), P * (h % 2)
+        return ("pb0", 0) if h == q else ("pb1", P * (h - q - 1))
+
+    def give_back(q, part, h0, h1):
+        least = min(len(topo.engines(cores[q], cores[x])) for x in range(q + 1, NR))
+        same = [h for h in range(h0, h1) if len(topo.engines(cores[q], cores[h])) > least]
+        far = [x for x in range(q + 1, NR) if x not in same] if len(same) == h1 - h0 else []
+        send(q, "f%d%d" % (q, part), [(h, "tu", 1024 * part + P * h, 1024 * part + P * h + P, "tin", P * (2 * q + part)) for h in range(h1 - 1, h0 - 1, -1)],
+             cfg["rem"] + 500 * (h1 - h0), far)
+
+    nv = [0] * NR
+
+    def task(q, r, st, h0, h1, h2):
+        n, w = P * (h1 - h0), W * (h1 - h0)
+        z = P * h0
+        c0 = 64 * r + W * h0
+        CS = ("csi", 0, 2056)
+        if r == 2 and max(h0, q + 1) < h1:
+            l0, l1 = W * max(h0, q + 1), W * h1
+            vec(q, lambda g, T: g.vector.tensor_scalar(T.es[:, 128 + l0:128 + l1], T.land[:, l0:l1], 65536.0 * (q + 1), None, A.min),
+                l1 - l0, [("land", l0, l1)], [("es", 128 + l0, 128 + l1)])
+        E, O1, O2 = ("es", c0, c0 + w), ("o1", c0, c0 + w), ("o2", c0, c0 + w)
+        shift = -7.5 / 16 + (8.0 - 4096.0 * q if q else 0.0)
+        y0 = 0 if q else 8
+        vec(q, lambda g, T: g.vector.tensor_scalar(T.o1[:, c0:c0 + w], T.es[:, c0:c0 + w], 1.0 / 16, shift, A.mult, A.add), w, [E], [O1])
+        act(q, lambda g, T: g.scalar.activation(T.d0[:, z:z + n:16], T.es[:, c0:c0 + w], AF.Identity if q else AF.Relu), w, [E], [("d0", z, z + n)])
+        vec(q, lambda g, T: g.vector.tensor_tensor(T.xx[:, z:z + n], T.yt[:, y0:4112].indirect(T.o1[:, c0:c0 + w]), T.wm[:, 0:n], A.mult), GAT * n,
+            [("yt", 0, 4112), O1, ("wm", 0, n)], [("xx", z, z + n)])
+        vec(q, lambda g, T: g.vector.tensor_tensor_scan(T.yy[:, z:z + n], T.d0[:, z:z + n], T.xx[:, z:z + n], -LOW, A.max, A.add), n,
+            [("d0", z, z + n), ("xx", z, z + n)], [("yy", z, z + n)])
+        vec(q, lambda g, T: g.vector.tensor_scalar(T.o2[:, c0:c0 + w], T.yy[:, z + 15:z + n:16], 1.0 / 32, LOW / 32 + 8, A.mult, A.add), w,
+            [("yy", z, z + n)], [O2])
+        if r == 5:
+            for h in range(h1 - 1, h0 - 1, -1):
+                c, x = 64 * r + W * h, 1024 + P * h
+                vec(q, lambda g, T, c=c, x=x: g.vector.tensor_copy(T.tu[:, x:x + P], T.csi[:, 0:2056].indirect(T.o2[:, c:c + W])), GAT * P,
+                    [CS, ("o2", c, c + W)], [("tu", x, x + P)])
+                give_back(q, 1, h, h + 1)
+            return
+        zc = z + 1024 * (r % 2)
+        if cfg["cs"][q]:
+            act(q, lambda g, T: g.scalar.activation(T.cg[:, zc:zc + n], T.csf[:, 0:2056].indirect(T.o2[:, c0:c0 + w]), AF.Copy), GAT * n,
+                [("csf", 0, 2056), O2], [("cg", zc, zc + n)])
+        if h2 < h1:
+            m, u = P * (h1 - h2), W * (h1 - h2)
+            c2, z2 = 64 * r + W * h2, zc + P * (h2 - h0)
+            S2, LS, CM, SE = ("o2", c2, c2 + u), ("lsb", 0, 2056), ("cmpb", z, z + m), ("selb", z, z + m)
+            x = vpos[(q, h2, event_of(q, h2, r))]
+            bv, bk = vbanks(q)[nv[q] % len(vbanks(q))], "pb%d" % (3 + st)
+            nv[q] += 1
+            pe(q, lambda g, T: g.tensor.matmul(T[bv][:, 0:m], T.g8h[0:8, :], T.vc[0:8, x:x + m], True, True), m, [("g8h", 0, 128), ("vc", x, x + m)], [(bv, 0, m)])
+            if cfg["cs"][q]:
+                vec(q, lambda g, T: g.vector.tensor_tensor(T.cmpb[:, z:z + m], T.cg[:, z2:z2 + m], T[bv][:, 0:m], A.is_le), m, [("cg", z2, z2 + m), (bv, 0, m)], [CM])
+            else:
+                act(q, lambda g, T: g.scalar.activation(T.vb[:, x:x + m], T[bv][:, 0:m], AF.Identity, bias=MID), m, [(bv, 0, m)], [("vb", x, x + m)])
+                vec(q, lambda g, T: g.vector.tensor_tensor(T.cmpb[:, z:z + m], T.csi[:, 0:2056].indirect(T.o2[:, c2:c2 + u]), T.vb[:, x:x + m], A.is_le), GAT * m,
+                    [CS, S2, ("vb", x, x + m)], [CM])
+            pe(q, lambda g, T: g.tensor.matmul(T[bk][:, 0:m], T.fb[:], T.cmpb[:, z:z + m], True, True), m, [("fb", 0, 128), CM], [(bk, 0, m)])
+            mb, m0 = (bk, 0) if cfg["ls"][q] else ("msk", z)
+            if cfg["mask"][q]:
+                act(q, lambda g, T: g.scalar.activation(T.ab[:, z:z + m], T[bk][:, 0:m], AF.Abs, bias=T.col[:, 4:5]), m, [(bk, 0, m), ("col", 4, 5)], [("ab", z, z + m)])
+                act(q, lambda g, T: g.scalar.activation(T[mb][:, m0:m0 + m], T.ab[:, z:z + m], AF.Relu, bias=1.0, scale=-1.0), m, [("ab", z, z + m)], [(mb, m0, m0 + m)])
+            else:
+                vec(q, lambda g, T: g.vector.tensor_scalar(T[mb][:, m0:m0 + m], T[bk][:, 0:m], T.col[:, 4:5], None, A.is_equal), m, [(bk, 0, m), ("col", 4, 5)], [(mb, m0, m0 + m)])
+            if cfg["ls"][q]:
+                act(q, lambda g, T: g.scalar.activation(T.lg[:, z:z + m], T.lsb[:, 0:2056].indirect(T.o2[:, c2:c2 + u]), AF.Copy), GAT * m, [LS, S2], [("lg", z, z + m)])
+                vec(q, lambda g, T: g.vector.tensor_tensor(T.selb[:, z:z + m], T.lg[:, z:z + m], T[bk][:, 0:m], A.mult), m, [("lg", z, z + m), (bk, 0, m)], [SE])
+            else:
+                vec(q, lambda g, T: g.vector.tensor_tensor(T.selb[:, z:z + m], T.lsb[:, 0:2056].indirect(T.o2[:, c2:c2 + u]), T.msk[:, z:z + m], A.mult), GAT * m,
+                    [LS, S2, ("msk", z, z + m)], [SE])
+            pe(q, lambda g, T: g.tensor.matmul(T[bk][:, 0:u], T.idn[:], T.es[:, c2:c2 + u], True, False), 256, [("idn", 0, 128), ("es", c2, c2 + u)], [(bk, 0, u)])
+
+            def wrap(g, T):
+                for i in range(16):
+                    last = g.tensor.matmul(T[bk][:, 0:u], T.hm[:, 16 - i:144 - i], T.selb[:, z + i:z + m:16], False, i == 15)
+                return last
+            pe(q, wrap, 1024, [("hm", 0, 144), SE], [(bk, 0, u)])
+            a, nx = h2, c2 + 64
+            if h2 == q:
+                act(q, lambda g, T: g.scalar.activation(T.es[:, nx:nx + W], T[bk][:, 0:W], AF.Copy), W, [(bk, 0, W)], [("es", nx, nx + W)])
+                a += 1
+                if q > 0:
+                    send(q, "r%d0%d" % (q, r), [(d, "es", nx, nx + W, "land", 64 * r + W * q) for d in (range(q - 1, -1, -1) if r == 0 else [q - 1])], cfg["rem"])
+            if a < h1:
+                t, lo, hi, e0 = r - 1, W * a, W * h1, 64 * r + 64
+                vec(q, lambda g, T: g.vector.tensor_tensor(T.es[:, e0 + lo:e0 + hi], T.land[:, 64 * t + lo:64 * t + hi], T[bk][:, lo - W * h2:hi - W * h2], A.min),
+                    hi - lo, [("land", 64 * t + lo, 64 * t + hi), (bk, 0, u)], [("es", e0 + lo, e0 + hi)])
+                if q > 0:
+                    send(q, "r%d%d%d" % (q, st, t), [(q - 1, "es", e0 + lo, e0 + hi, "land", 64 * t + lo)], cfg["rem"])
+        b, x0 = tally_at(q, h0)
+        if cfg["cs"][q]:
+            for k in range(0, n, cfg["tw"]):
+                me, e = len(ops), k + cfg["tw"]
+                pe(q, lambda g, T, me=me, k=k, e=e: g.tensor.matmul(T[b][:, x0 + k:x0 + e], T.idn[:], T.cg[:, zc + k:zc + e], False, closing[(q, b)] == me), 4 * (e - k),
+                   [("idn", 0, 128), ("cg", zc + k, zc + e)], [(b, x0 + k, x0 + e)])
+                ops[me]["sum"] = b
+        elif r == (0 if h0 == q else 2):
+            vec(q, lambda g, T: g.vector.tensor_copy(T.tl[:, x0:x0 + n], T.csi[:, 0:2056].indirect(T.o2[:, c0:c0 + w])), GAT * n, [CS, O2], [("tl", x0, x0 + n)])
+        else:
+            vec(q, lambda g, T: g.vector.tensor_tensor(T.tl[:, x0:x0 + n], T.csi[:, 0:2056].indirect(T.o2[:, c0:c0 + w]), T.tl[:, x0:x0 + n], A.add), GAT * n,
+                [CS, O2, ("tl", x0, x0 + n)], [("tl", x0, x0 + n)])
+
+    def partial(q):
+        for (a, b) in ((1, 2), (2, NR)) if q == 0 else ((q + 1, NR),):
+            bf, x = tally_at(q, a)
+            n = P * (b - a)
+            vec(q, lambda g, T, a=a, b=b, bf=bf, x=x, n=n: g.vector.tensor_scalar(T.tu[:, P * a:P * b], T[bf][:, x:x + n], 3 * MID * cfg["cs"][q], None, A.add),
+                n, [(bf, x, x + n)], [("tu", P * a, P * b)])
+            give_back(q, 0, a, b)
+
+    def finish(q):
+        b, x = tally_at(q, q)
+        if cfg["cs"][q]:
+            act(q, lambda g, T, b=b, x=x: g.scalar.activation(T.acc[:, 0:P], T[b][:, x:x + P], AF.Identity, bias=5 * MID), P, [(b, x, x + P)], [("acc", 0, P)])
+            b, x = "acc", 0
+        k = 0
+        for part in range(2):
+            for s in range(q - 1, -1, -1):
+                pb, i0 = "pb%d" % (6 + k % 2), P * (2 * s + part)
+                k += 1
+                o = P * k
+                vec(q, lambda g, T, i0=i0, pb=pb: g.vector.tensor_copy(T[pb][:, 0:P], T.tin[:, i0:i0 + P]), P, [("tin", i0, i0 + P)], [(pb, 0, P)])
+                vec(q, lambda g, T, b=b, x=x, pb=pb, o=o: g.vector.tensor_tensor(T.acc[:, o:o + P], T[b][:, x:x + P], T[pb][:, 0:P], A.add), P,
+                    [(b, x, x + P), (pb, 0, P)], [("acc", o, o + P)])
+                b, x = "acc", o
+        dma(q, "s", lambda g, T: g.sync.dma_start(T.y[:], T[b][:, x:x + P]), 2500, [(b, x, x + P)], [("y", 0, 1)])
+
+    for q in range(NR):
+        start(q)
+    for rnd in range(6):
+        for q in range(NR - 1, -1, -1):
+            if rnd == 5 and q < NR - 1:
+                partial(q)
+            for tk in TASKS[q]:
+                if tk[0] == rnd:
+                    tag[0] = "%d%d%d" % (q, tk[0], tk[1])
+                    task(q, *tk)
+                    tag[0] = None
+            if rnd == 0:
+                visitors_v(q)
+    for q in range(NR):
+        finish(q)
+
+    share = {}
+    for i, o in enumerate(ops):
+        if o["sem"]:
+            share.setdefault((o["q"], o["sem"][0]), []).append(i)
+    for o in ops:
+        for j in list(o["deps"]):
+            if ops[j]["sem"]:
+                o["deps"].update(share[(ops[j]["q"], ops[j]["sem"][0])])
+
+    n = len(ops)
+    users = [[] for _ in range(n)]
+    for i, o in enumerate(ops):
+        for j in o["deps"]:
+            users[j].append(i)
+    tail = [0.0] * n
+    for i in range(n - 1, -1, -1):
+        tail[i] = ops[i]["busy"] + ops[i]["lat"] + max([tail[u] + HOP for u in users[i]] + [0.0])
+    seed = cfg["seed"]
+    for i in range(n):
+        seed = (seed * 1103515245 + 12345) % 2147483648
+        tail[i] += cfg["prio"].get(ops[i]["tag"], 0.0) + ops[i].get("boost", 0.0) + cfg["noise"] * seed / 2147483648
+    left = [len(o["deps"]) for o in ops]
+    ready = [i for i in range(n) if left[i] == 0]
+    can, free, order, end = [0.0] * n, {}, [], 0.0
+    while ready:
+        st = {i: max(can[i], free.get((ops[i]["q"], ops[i]["e"]), 0.0)) for i in ready}
+        i0 = min(ready, key=lambda i: (st[i], i))
+        key = (ops[i0]["q"], ops[i0]["e"])
+        near = [i for i in ready if (ops[i]["q"], ops[i]["e"]) == key and st[i] <= st[i0] + min(cfg["look"], cfg["lk2"] * ops[i0]["busy"])
+                and (i == i0 or tail[i] > tail[i0] + cfg["marg"])]
+        i = max(near, key=lambda i: (tail[i], -i))
+        ready.remove(i)
+        o = ops[i]
+        o["t"] = st[i]
+        free[key] = st[i] + o["busy"]
+        done = free[key] + o["lat"]
+        end = max(end, done)
+        order.append(i)
+        for u in users[i]:
+            same = o["e"] == ops[u]["e"] and o["q"] == ops[u]["q"] and o["e"] == "p"
+            can[u] = max(can[u], done + (0.0 if same else HOP))
+            left[u] -= 1
+            if left[u] == 0:
+                ready.append(u)
+    count = {}
+    for i in order:
+        o = ops[i]
+        if "sum" in o:
+            closing[(o["q"], o["sum"])] = i
+        if o["sem"]:
+            o["sig"] = o["sem"]
+        elif not o["rem"]:
+            key = (o["q"], o["e"])
+            count[key] = count.get(key, 0) + 1
+            o["sig"] = (COUNT[o["e"]], count[key])
+    return ops, order, end
+
+
+PLAN = {}
+
+
+def rank_program(g, core, T, topo):
+    q = T.rank_of(core)
+    if q is None:
+        return
+    if "p" not in PLAN:
+        PLAN["p"] = build(list(T.cores), topo, CFG)
+    ops, order, _ = PLAN["p"]
+    queue = {"g": g, "v": g.vector, "a": g.scalar, "p": g.tensor, "s": g.sync}
+    seen, total = {}, {}
+    for i in order:
+        o = ops[i]
+        if o["rem"] and q in o["rem"][1]:
+            total[o["rem"][0]] = total.get(o["rem"][0], 0) + o["rem"][1][q]
+        if o["q"] != q:
+            continue
+        need = {}
+        for j in o["deps"]:
+            d = ops[j]
+            if d["rem"]:
+                s, v = d["rem"][0], d["rem"][1][q]
+            elif d["e"] == "p" and o["e"] == "p":
+                continue
+            elif d["e"] == "g" and o["e"] == "g" and d["w"][0] != "f0":
+                continue
+            else:
+                s, v = d["sig"]
+            need[s] = max(need.get(s, 0), v)
+        for s, v in need.items():
+            if seen.get((o["e"], s), 0) < v:
+                seen[(o["e"], s)] = v
+                queue[o["e"]].wait_ge(T.sem[s], v)
+        r = o["fn"](g, T)
+        if o["rem"]:
+            total["sent"] = total.get("sent", 0) + sum(o["rem"][1].values())
+        else:
+            r.then_inc(T.sem[o["sig"][0]], 16 if o["sem"] else 1)
+            total[o["sig"][0]] = o["sig"][1]
+    for s, v in total.items():
+        if seen.get(("g", s), 0) < v:
+            g.wait_ge(T.sem[s], v)

@@ -2,98 +2,149 @@ from concourse.bass import DstId, RemoteDMATransfer
 from concourse.mybir import AluOpType as A, ActivationFunctionType as AF
 
 NR, P, W = 4, 256, 16
-BIG, LOW, MID = float(1 << 22), float(1 << 19), 2048.0
+BIG, HUGE, OUT, CAP, MID = float(1 << 20), float(1 << 22), float(1 << 19), float(1 << 18), 2048.0
 CFG = {
-    "bm": (0, 0, 0, 0), "cs": (1, 0, 0, 0), "ls": (0, 1, 1, 1), "mask": (1, 0, 0, 0),
-    "streams": (((0, 1), (1, 2), (2, 3), (3, 4)), ((1, 2), (2, 3), (3, 4)), ((2, 3), (3, 4)), ((3, 4),)),
-    "cyc": 1.04, "gat": 1.56, "hop": 110.0, "pe": 0.52, "rem": 2500.0, "t_cs": 6500.0, "t_ls": 8500.0,
-    "look": 100.0, "lk2": 0.5, "marg": 1000.0, "seed": 1, "noise": 0.0, "tw": 256,
-    "prio": {"210": -300, "021": -1500, "121": 1500, "240": -1500, "011": -3000, "120": -1500, "040": 300, "140": -1200,
-             "142": -1100, "221": -1500, "042": 1000, "041": -3000, "131": 300, "241": -3000, "031": -700, "230": 1500,
-             "043": -3000, "130": 2700, "122": -700, "020": -1500, "152": -1500, "032": 3000, "000": 700, "010": 700},
+    "streams": (((0, 256, 2, 2, "aaaa"), (256, 512, 3, 3, "aaaa"), (512, 768, 4, 4, "aaaa"), (768, 1024, 5, 6, "aaaa")),
+                ((256, 512, 2, 3, "aaaa"), (512, 768, 4, 5, "aaaa"), (768, 1024, 6, 7, "aaav")),
+                ((512, 768, 2, 3, "avav"), (768, 1024, 4, 5, "avav")),
+                ((768, 1024, 2, 3, "avav"),)),
+    "direct": True, "evac": ("aavaaaav", "avavavav", "avavavav", "avavavav"), "cast": False, "once": False,
+    "apart": 0, "leave": False, "one": 7,
+    "whole": ((1,), (), (), ()), "early": ((1,), (), (), ()),
+    "fix": 50.0, "pfix": 10.0, "cyc": 0.88, "gat": 1.56, "hop": 100.0, "pe": 0.45, "rem": 1200.0, "row": 50.0, "byte": 0.06,
+    "issue": 500.0, "first": 1500.0, "fresh": 100.0, "t_in": 2000.0, "t_cs": 5800.0,
+    "t_ls": 7200.0, "t_g": 1000.0, "t_cast": 4000.0, "look": (60.0, 60.0, 60.0, 60.0), "prio": {}, "seed": 1, "tries": 500, "slack": 200.0,
 }
 
 F, I, H, B, U = "float32", "int32", "float16", "bfloat16", "uint16"
 SCRATCH = {k: ("sbuf", [128, n], t) for k, n, t in (
-    ("bmc", 512, I), ("bmt", 512, I), ("cc", 256, F), ("hl", 512, H), ("yt", 4112, F), ("csi", 2056, I), ("csf", 2056, F),
-    ("lsb", 2064, B), ("ia", 128, I), ("ib", 128, I), ("ibh", 128, H), ("sm", 1024, H), ("ones", 128, F), ("f0", 128, F),
-    ("f1", 128, F), ("fb", 128, B), ("hm", 144, B), ("zb", 512, B), ("idn", 128, F), ("g8", 128, F), ("g8h", 128, H),
-    ("i16", 32, I), ("j16", 32, I), ("col", 32, F), ("wm", 512, F), ("d0", 1024, F), ("sdi", 16, I), ("vi", 64, I),
-    ("vf", 64, H), ("vl", 192, H), ("vc", 3328, H), ("vb", 3328, F), ("eni", 32, I), ("enf", 32, F), ("ent", 32, F),
-    ("enm", 32, F), ("es", 384, F), ("land", 256, F), ("o1", 384, U), ("o2", 384, U), ("xx", 1024, F), ("yy", 1024, F),
-    ("cg", 2048, F), ("ab", 1024, F), ("lg", 1024, B), ("cmpb", 1024, B), ("msk", 1024, B), ("selb", 1024, B),
-    ("tl", 1024, F), ("tu", 2048, U), ("tin", 1536, U), ("acc", 2048, F))}
+    ("bmc", 512, I), ("bmt", 512, I), ("cc", 256, F), ("hl", 512, H), ("yt", 4112, F), ("csi", 2064, I), ("csf", 2064, F),
+    ("lsb", 2064, B), ("ia", 128, I), ("ib", 128, I), ("ibh", 128, H), ("sm", 1024, H), ("ones", 128, F), ("rr", 128, F),
+    ("r1", 128, B), ("r2", 128, B), ("r3", 128, F), ("r4", 128, B), ("t1", 128, B), ("t2", 128, B), ("t4", 128, B),
+    ("wk", 128, B), ("wy", 128, B), ("wc", 128, B), ("idb", 128, B), ("zb", 128, B), ("idn", 128, F), ("g8", 128, F),
+    ("g8h", 128, H), ("onb", 512, B), ("mid", 128, B), ("i16", 16, I), ("j16", 16, I), ("j1", 8, I), ("col", 128, F),
+    ("da", 16, F), ("db", 16, F), ("dd", 1024, F), ("oz", 8, U), ("zi", 16, F), ("zl", 16, B), ("sdi", 16, I), ("vi", 64, I),
+    ("vf", 64, H), ("vc", 4096, H), ("vb", 1024, F), ("eni", 32, I), ("enf", 32, F), ("ent", 32, F),
+    ("enm", 32, F), ("es", 384, F), ("land", 256, F), ("mine", 64, F), ("more", 256, F), ("o1", 384, U), ("o2", 384, U),
+    ("xx", 1024, F), ("y1", 1024, F), ("y2", 1024, F), ("cg", 2048, F), ("lg", 1024, B), ("cmpb", 1024, B), ("yb", 1024, B),
+    ("tu", 2048, U), ("tin", 1536, U), ("tf", 1536, F), ("acc", 512, F))}
+for _h in range(1, NR):
+    SCRATCH["vd%d" % _h] = ("dram", [128, 64], H)
 for _b in range(8):
     SCRATCH["pb%d" % _b] = ("psum", [128, 512], F)
 
-SEMAPHORES = (["nv", "na", "nt", "ng", "sent"] + ["d%d" % i for i in range(14)] + ["v%d" % h for h in range(NR)]
-              + ["r%d%d%d" % (s, k, t) for s in range(1, NR) for k in range(3) for t in range(4)]
-              + ["f%d%d" % (s, k) for s in range(NR) for k in range(2)])
+SEMAPHORES = ["nv", "na", "nt", "ng", "sent"] + ["d%d" % i for i in range(32)] + ["m%d" % i for i in range(60)]
 COUNT = {"v": "nv", "a": "na", "p": "nt", "g": "ng"}
+CALLS = {
+    "set": lambda g, o, c: g.vector.memset(o, c),
+    "cp": lambda g, o, i: g.vector.tensor_copy(o, i),
+    "tt": lambda g, o, a, b, op: g.vector.tensor_tensor(o, a, b, op),
+    "ts1": lambda g, o, a, s, op: g.vector.tensor_scalar(o, a, s, None, op),
+    "ts2": lambda g, o, a, s1, s2, op0, op1: g.vector.tensor_scalar(o, a, s1, s2, op0, op1),
+    "scan": lambda g, o, a, b: g.vector.tensor_tensor_scan(o, a, b, HUGE, A.min, A.add),
+    "tr": lambda g, o, i: g.vector.transpose(o, i),
+    "acp": lambda g, o, i, s: g.scalar.activation(o, i, AF.Copy, scale=s),
+    "aid": lambda g, o, i, b, s: g.scalar.activation(o, i, AF.Identity, bias=b, scale=s),
+    "sign": lambda g, o, i: g.scalar.activation(o, i, AF.Sign),
+    "mm": lambda g, o, l, r, start, stop: g.tensor.matmul(o, l, r, start, stop),
+    "iota": lambda g, o, pat, base, cm: g.iota(o, pat, base, cm),
+    "iotaf": lambda g, o, pat, base, cm: g.iota(o, pat, base, cm, allow_small_or_imprecise_dtypes=True),
+    "sel": lambda g, o, i, pat, op, base, cm: g.affine_select(o, i, pat, op, 0.0, base, cm),
+    "g": lambda g, o, i: g.dma_start(o, i),
+    "s": lambda g, o, i: g.sync.dma_start(o, i),
+    "a": lambda g, o, i: g.scalar.dma_start(o, i),
+}
 
 
-def tasks_of(q, streams):
-    out = [(0, 0, q, q + 1, q), (1, 0, q, q + 1, q)]
-    for r in range(2, 6):
-        for st in range(len(streams) - 1, -1, -1):
-            a, b = streams[st]
-            if r == 5:
-                a = max(a, q + 1)
-                if a < b:
-                    out.append((r, st, a, b, b))
-            else:
-                out.append((r, st, a, b, max(a, q + 1) if r == 4 else a))
-    return out
+def ap(name, lo, hi, step=1, rows=(0, 128)):
+    return (name, lo, hi, step, rows[0], rows[1])
 
 
-def event_of(q, h, r):
-    return r if h == q else r - 1
+def ind(win, off):
+    return ("@", win, off)
+
+
+def col(k, rows=(0, 128)):
+    return ap("col", 4 * k, 4 * k + 1, 1, rows)
+
+
+def last(name, lo, hi):
+    return ap(name, lo + W - 1, hi, W)
+
+
+def wrapped(name, k, lo, hi):
+    return ap(name, 64 * k + lo // W, 64 * k + hi // W)
+
+
+def real(T, a):
+    if not isinstance(a, tuple):
+        return a
+    if a[0] == "@":
+        return real(T, a[1]).indirect(real(T, a[2]))
+    return T[a[0]][a[4]:a[5], a[1]:a[2]:a[3]] if a[3] > 1 else T[a[0]][a[4]:a[5], a[1]:a[2]]
+
+
+def parts(a):
+    return [] if not isinstance(a, tuple) else [a[1], a[2]] if a[0] == "@" else [a]
 
 
 def build(cores, topo, cfg):
-    ops, hist = [], {}
-    CYC, GAT, HOP = cfg["cyc"], cfg["gat"], cfg["hop"]
-    TASKS = [tasks_of(q, cfg["streams"][q]) for q in range(NR)]
-    closing, tag = {}, [None]
+    ops, hist, late = [], {}, []
+    CYC, GAT, HOP, CAST = cfg["cyc"], cfg["gat"], cfg["hop"], cfg["cast"]
+    LESS = 0.0 if CAST else MID
+    tag, ndma, nmsg = [None], [0] * NR, [0] * NR
 
-    def add(q, eng, fn, busy, rd=(), wr=(), lat=0.0, sem=None, remote=None):
-        i = len(ops)
-        deps = set()
+    def add(q, eng, kind, args, busy, rd, wr, lat=0.0, sem=None, remote=None):
+        i, deps = len(ops), set()
         for acc, write in ((rd, False), (wr, True)):
-            for a in acc:
-                r, name, lo, hi = a if len(a) == 4 else (q,) + tuple(a)
-                for (j, e2, l2, h2, w2) in hist.setdefault((r, name), []):
-                    if j == i:
-                        continue
-                    meet = lo < h2 and l2 < hi and (write or w2)
-                    if meet or (name.startswith("pb") and e2 != eng):
+            for r, (name, lo, hi, _, r0, r1) in acc:
+                for (j, e2, l2, h2, a2, b2, w2) in hist.setdefault((r, name), []):
+                    meet = lo < h2 and l2 < hi and r0 < b2 and a2 < r1 and (write or w2)
+                    if j != i and (meet or (name.startswith("pb") and e2 != eng)):
                         deps.add(j)
-                hist[(r, name)].append((i, eng, lo, hi, write))
-        ops.append({"q": q, "e": eng, "fn": fn, "busy": busy, "lat": lat, "deps": deps, "sem": sem, "rem": remote,
-                    "w": list(wr)[0], "tag": tag[0]})
+                hist[(r, name)].append((i, eng, lo, hi, r0, r1, write))
+        ops.append({"q": q, "e": eng, "kind": kind, "args": list(args), "busy": busy, "lat": lat, "deps": deps, "sem": sem,
+                    "rem": remote, "name": wr[0][1][0], "tag": tag[0]})
         return i
 
-    def vec(q, fn, cyc, rd, wr):
-        return add(q, "v", fn, 45 + max(64, cyc) * CYC, rd, wr)
+    def call(q, eng, kind, args, busy, **kw):
+        rd = [(q, x) for a in args[1:] for x in parts(a)]
+        return add(q, eng, kind, args, busy, rd, [(q, args[0])], **kw)
 
-    def act(q, fn, cyc, rd, wr):
-        return add(q, "a", fn, 60 + max(64, cyc) * CYC, rd, wr)
+    def width(a):
+        return W * width(a[2]) * GAT if a[0] == "@" else (a[2] - a[1] + a[3] - 1) // a[3]
 
-    def pe(q, fn, cyc, rd, wr):
-        return add(q, "p", fn, 30 + cyc * cfg["pe"], rd, wr)
+    def vec(q, kind, *args):
+        n = width(args[0] if kind == "set" else args[1])
+        if kind == "tt" and args[1][0] != "@" and not (args[1][0].startswith("pb") or args[2][0].startswith("pb")):
+            n *= 2
+        return call(q, "v", kind, args, cfg["fix"] + max(64, n) * CYC)
 
-    def gp(q, fn, n, rd, wr):
-        return add(q, "g", fn, 150 + 2 * n * CYC, rd, list(wr) + [("order", 0, 1)])
+    def act(q, out, src, bias=None, scale=1.0):
+        busy = cfg["fix"] + 15 + max(64, width(src)) * CYC
+        return call(q, "a", "acp", (out, src, scale), busy) if bias is None else call(q, "a", "aid", (out, src, bias, scale), busy)
 
-    def fill(q, name, sl, n, c, reg, rows=slice(0, 128)):
-        return act(q, lambda g, T: g.scalar.activation(T[name][rows, sl], T.ones[rows, 0:n], AF.Copy, scale=c), n, [("ones", 0, 128)], [reg])
+    def mm(q, out, lhs, rhs, start, stop):
+        slow = 4 if SCRATCH[rhs[0]][2] == F else 1
+        return call(q, "p", "mm", (out, lhs, rhs, start, stop), cfg["pfix"] + max(64, width(rhs)) * slow * cfg["pe"], lat=40.0)
 
-    ndma = [0] * NR
+    def gp(q, kind, *args):
+        rd = [(q, x) for a in args[1:] for x in parts(a)]
+        return add(q, "g", kind, args, 150 + 2 * width(args[0]) * CYC, rd, [(q, args[0]), (q, ap("order", 0, 1))])
 
-    def dma(q, eng, fn, lat, rd, wr):
+    def fill(q, out, c):
+        return act(q, out, ap("ones", 0, width(out), 1, out[4:6]), None, c)
+
+    def gather(q, eng, out, win, off, plus=None):
+        if eng == "a":
+            return act(q, out, ind(win, off))
+        return vec(q, "cp", out, ind(win, off)) if not plus else vec(q, "ts1", out, ind(win, off), plus, A.add)
+
+    def dma(q, eng, out, src, lat, boost=False):
         ndma[q] += 1
-        i = add(q, eng, fn, 80, rd, wr, lat=lat, sem=("d%d" % (ndma[q] - 1), 16))
-        ops[i]["boost"] = 1e6 - 1e4 * ndma[q]
+        i = add(q, eng, eng, (out, src), 80, [(q, src)], [(q, out)], lat=lat, sem=("d%d" % (ndma[q] - 1), 16))
+        if boost:
+            ops[i]["boost"] = 1e6 - 1e4 * ndma[q]
         return i
 
     def split_engines(q, dsts, leave):
@@ -113,288 +164,317 @@ def build(cores, topo, cfg):
                     used.update(res[d])
         return res
 
-    def send(q, sem, items, lat, leave=()):
+    def send(q, items, leave=()):
         eng = split_engines(q, [it[0] for it in items], leave)
+        sig, tr = {}, []
+        for d, src, dst in items:
+            nmsg[d] += 1
+            sig[d] = ("m%d" % (nmsg[d] - 1), len(eng[d]))
+            tr.append([cores[d], sum(1 << e for e in eng[d]), sig[d][0], src, dst])
+        size = (items[0][1][2] - items[0][1][1]) * (4 if SCRATCH[items[0][1][0]][2] == F else 2)
+        lats = {d: cfg["rem"] + 128 / len(e) * (cfg["row"] + size * cfg["byte"]) for d, e in eng.items()}
+        i = add(q, "g", "send", (cores[q], tr), cfg["issue"], [(q, it[1]) for it in items], [(it[0], it[2]) for it in items],
+                lat=max(lats.values()), remote=sig)
+        ops[i]["lats"], ops[i]["uses"] = lats, {e for v in eng.values() for e in v}
+        return i
 
-        def fn(g, T):
-            tr = []
-            for (d, sb, lo, hi, db, dlo) in items:
-                rid, pid = topo.addr(cores[d], cores[q])
-                tr.append(RemoteDMATransfer(dst_ids=[DstId(rid=rid, pnc=pid)], dma_engine_mask=sum(1 << e for e in eng[d]),
-                                            remote_sem=T.sem[sem], src=T[sb][:, lo:hi], dst=T[db][:, dlo:dlo + hi - lo]))
-            g.remote_dma_fused(tr, local_sem=T.sem.sent)
-            return None
-        return add(q, "g", fn, 500, [(it[1], it[2], it[3]) for it in items],
-                   [(it[0], it[4], it[5], it[5] + it[3] - it[2]) for it in items], lat=lat,
-                   remote=(sem, {d: len(e) for d, e in eng.items()}))
+    (C_W, C_ODD, C_EVEN, C_LOW, C_16, C_T, C_K1, C_K2, C_TOP, C_S1, C_S2, C_WC, C_END) = range(13)
+    FIRST, FIN = ap("db", 15, 16), ap("da", 15, 16)
+    LO, HI, EIGHT = (0, 64), (64, 128), (0, 8)
+    CSI, CSF, LS = ap("csi", 0, 2064), ap("csf", 0, 2064), ap("lsb", 0, 2064)
 
-    vpos = {}
-    for q in range(NR):
-        n = 0
-        for (r, _, h0, h1, h2) in TASKS[q]:
-            for h in range(h2, h1):
-                vpos[(q, h, event_of(q, h, r))] = n
-                n += P
-
-    def vbanks(q):
-        return ["pb%d" % b for b in range(3 + len(cfg["streams"][q]), 8)] + ["pb2"]
+    def floats(q):
+        return any(s[4][1] != "v" for s in cfg["streams"][q])
 
     def start(q):
-        wide = P * max(b - a for a, b in cfg["streams"][q])
-        one = [("ones", 0, 128)]
-        dma(q, "s", lambda g, T: g.sync.dma_start(T.bmc[0:64, :], T.bm[:]), 2000, [], [("bmc0", 0, 1)])
-        dma(q, "a", lambda g, T: g.scalar.dma_start(T.bmc[64:128, :], T.bm[:]), 2000, [], [("bmc1", 0, 1)])
-        dma(q, "a", lambda g, T: g.scalar.dma_start(T.sdi[:], T.sd[:]), 2000, [], [("sdi", 0, 16)])
-        dma(q, "s", lambda g, T: g.sync.dma_start(T.eni[:, 0:16], T.en[:]), 2100, [], [("eni", 0, 16)])
-        dma(q, "a", lambda g, T: g.scalar.dma_start(T.eni[:, 16:32], T.en[:]), 2100, [], [("eni", 16, 32)])
-        dma(q, "s", lambda g, T: g.sync.dma_start(T.csi[:, 8:2056], T.cs[:]), cfg["t_cs"], [], [("csi", 8, 2056)])
-        dma(q, "s", lambda g, T: g.sync.dma_start(T.lsb[:, 8:2056], T.ls[:]), cfg["t_ls"], [], [("lsb", 8, 2056)])
-        vec(q, lambda g, T: g.vector.memset(T.ones[:], 1.0), 128, [], one)
-        gp(q, lambda g, T: g.iota(T.ia[:], [[-8, 8], [0, 16]], 64, 1), 128, [], [("ia", 0, 128)])
-        gp(q, lambda g, T: g.iota(T.i16[:, 0:17], [[-1, 17]], 16, 1), 17, [], [("i16", 0, 17)])
-        gp(q, lambda g, T: g.iota(T.cc[:], [[-1, 256]], 0, 0, allow_small_or_imprecise_dtypes=True), 256, [], [("cc", 0, 256)])
-        gp(q, lambda g, T: g.affine_select(T.g8[0:8, :], T.ones[0:8, :], [[-1, 8], [0, 16]], A.is_equal, 0.0, 0, 1), 128, one, [("g8", 0, 128)])
-        gp(q, lambda g, T: g.affine_select(T.f0[:], T.ones[:], [[-16, 8], [0, 16]], A.is_ge, 0.0, 0, 1), 128, one, [("f0", 0, 128)])
-        gp(q, lambda g, T: g.affine_select(T.f1[:], T.f0[:], [[16, 8], [0, 16]], A.is_ge, 0.0, 15, -1), 128, [("f0", 0, 128)], [("f1", 0, 128)])
-        gp(q, lambda g, T: g.affine_select(T.idn[:], T.ones[:], [[-1, 128]], A.is_equal, 0.0, 0, 1), 128, one, [("idn", 0, 128)])
-        vec(q, lambda g, T: g.vector.tensor_copy(T.g8h[0:8, :], T.g8[0:8, :]), 128, [("g8", 0, 128)], [("g8h", 0, 128)])
-        fill(q, "col", slice(0, 1), 1, 32.0, ("colA", 0, 1), slice(0, 64))
-        fill(q, "col", slice(0, 1), 1, -1.0, ("colB", 0, 1), slice(64, 128))
-        vec(q, lambda g, T: g.vector.tensor_scalar(T.ib[:], T.ia[:], 63, None, A.bitwise_and), 128, [("ia", 0, 128)], [("ib", 0, 128)])
-        vec(q, lambda g, T: g.vector.tensor_copy(T.ibh[:], T.ib[:]), 128, [("ib", 0, 128)], [("ibh", 0, 128)])
+        one, begin, z = ap("ones", 0, 128), len(ops), P * (NR - 1)
+        t0 = cfg["t_in"]
+        dma(q, "s", ap("bmc", 0, 512, 1, LO), ap("bm", 0, 4096, 1, EIGHT), t0, True)
+        if not cfg["once"]:
+            dma(q, "a", ap("bmc", 0, 512, 1, HI), ap("bm", 0, 4096, 1, EIGHT), t0, True)
+        dma(q, "a", ap("sdi", 0, 16), ap("sd", 0, P, 1, EIGHT), t0, True)
+        dma(q, "s", ap("eni", 0, 16), ap("en", 0, P, 1, EIGHT), t0 + 100, True)
+        dma(q, "a", ap("eni", 16, 32), ap("en", 0, P, 1, EIGHT), t0 + 100, True)
+        dma(q, "s", ap("csi", 8, 2056), ap("cs", 0, 2048), cfg["t_cs"], True)
+        loaded = dma(q, "s", ap("lsb", 8, 2056), ap("ls", 0, 2048), cfg["t_ls"], True)
+        vec(q, "set", one, 1.0)
+        fill(q, ap("zb", 0, 128), 0.0)
+
+        def blocks(out, tmp, src):
+            gp(q, "sel", ap(tmp, 0, 128), src, [[-16, 8], [0, 16]], A.is_ge, 0, 1)
+            gp(q, "sel", ap(out, 0, 128), ap(tmp, 0, 128), [[16, 8], [0, 16]], A.is_ge, 15, -1)
+        gp(q, "iota", ap("ia", 0, 128), [[-8, 8], [0, 16]], 64, 1)
+        gp(q, "iota", ap("i16", 0, 16), [[-1, 16]], 16, 1)
+        gp(q, "sel", ap("g8", 0, 128, 1, EIGHT), ap("ones", 0, 128, 1, EIGHT), [[-1, 8], [0, 16]], A.is_equal, 0, 1)
+        gp(q, "iotaf", ap("cc", 0, 256), [[-1, 256]], 0, 0)
+        gp(q, "iotaf", ap("rr", 0, 128), [[0, 8], [1, 16]], -15, 0)
+        gp(q, "sel", ap("idn", 0, 128), one, [[-1, 128]], A.is_equal, 0, 1)
+        if CAST:
+            vec(q, "set", ap("onb", 0, P, 1, (0, 1)), 1.0)
+            fill(q, ap("mid", 0, 128, 1, (0, 1)), MID)
+        fill(q, col(C_W, LO), 32.0)
+        fill(q, col(C_W, HI), -1.0)
+        fill(q, col(C_LOW, LO), 1.0)
+        fill(q, col(C_LOW, HI), 0.0)
+        act(q, col(C_16), col(C_LOW), 16.0, -16.0)
+        vec(q, "ts1", ap("ib", 0, 128), ap("ia", 0, 128), 63, A.bitwise_and)
+        vec(q, "cp", ap("ibh", 0, 128), ap("ib", 0, 128))
         for o in range(8):
-            vec(q, lambda g, T, o=o: g.vector.tensor_scalar(T.sm[:, 128 * o:128 * o + 128], T.ibh[:], float(o), T.col[:, 0:1], A.is_equal, A.mult),
-                64, [("ibh", 0, 128), ("colA", 0, 1), ("colB", 0, 1)], [("sm", 128 * o, 128 * o + 128)])
-        act(q, lambda g, T: g.scalar.activation(T.fb[:], T.f1[:], AF.Copy), 128, [("f1", 0, 128)], [("fb", 0, 128)])
-        fill(q, "hm", slice(0, 128), 128, 0.0, ("hm", 0, 128))
-        fill(q, "hm", slice(128, 144), 16, 0.0, ("hm", 128, 144))
-        act(q, lambda g, T: g.scalar.activation(T.hm[:, 16:144:16], T.f1[:, 0:128:16], AF.Copy, scale=-1.0), 8, [("f1", 0, 128)], [("hm", 0, 144)])
-        vec(q, lambda g, T: g.vector.tensor_scalar(T.j16[:, 0:16], T.i16[:, 0:16], 15, None, A.bitwise_and), 16, [("i16", 0, 17)], [("j16", 0, 16)])
-        vec(q, lambda g, T: g.vector.tensor_scalar(T.j16[:, 16:17], T.i16[:, 16:17], 4, 1, A.logical_shift_right, A.bitwise_and), 1, [("i16", 0, 17)], [("j16", 16, 17)])
-        vec(q, lambda g, T: g.vector.tensor_scalar(T.wm[:, 0:16], T.j16[:, 0:16], 0.0, None, A.is_equal), 16, [("j16", 0, 16)], [("wm", 0, 16)])
-        sg = -1.0 if cfg["mask"][q] else 1.0
-        vec(q, lambda g, T: g.vector.tensor_scalar(T.col[:, 4:5], T.j16[:, 0:1], sg, None, A.mult), 1, [("j16", 0, 16)], [("col", 4, 5)])
-        vec(q, lambda g, T: g.vector.tensor_copy(T.col[:, 8:9], T.j16[:, 16:17]), 1, [("j16", 16, 17)], [("col", 8, 9)])
-        act(q, lambda g, T: g.scalar.activation(T.col[:, 12:13], T.col[:, 8:9], AF.Identity, bias=1.0, scale=-1.0), 1, [("col", 8, 9)], [("col", 12, 13)])
-        n = 16
-        while n < wide:
-            act(q, lambda g, T, n=n: g.scalar.activation(T.wm[:, n:2 * n], T.wm[:, 0:n], AF.Copy), n, [("wm", 0, n)], [("wm", n, 2 * n)])
-            n *= 2
-        for x in range(P * q, P * NR, 128):
-            fill(q, "d0", slice(x, x + 128), 128, -BIG, ("d0", x, x + 128))
-        if q > 0:
-            fill(q, "yt", slice(0, 8), 8, -BIG, ("yt", 0, 8))
-        fill(q, "yt", slice(4104, 4112), 8, -BIG, ("yt", 4104, 4112))
-        vec(q, lambda g, T: g.vector.memset(T.csi[:, 0:8], 0), 8, [], [("csi", 0, 8)])
-        fill(q, "lsb", slice(0, 8), 8, 0.0, ("lsb", 0, 8))
-        for t in range(4):
-            vec(q, lambda g, T, t=t: g.vector.tensor_scalar(T.vi[:, 16 * t:16 * t + 16], T.sdi[:], 4 * t, 4095, A.logical_shift_right, A.bitwise_and),
-                16, [("sdi", 0, 16)], [("vi", 16 * t, 16 * t + 16)])
-        vec(q, lambda g, T: g.vector.tensor_scalar(T.vf[:], T.vi[:], -MID, None, A.add), 64, [("vi", 0, 64)], [("vf", 0, 64)])
-        for t in range(4):
-            x = vpos[(q, q, t)]
-            add(q, "s", lambda g, T, t=t, x=x: g.sync.dma_start(T.vc[0:8, x:x + P], T.vf[:, 16 * t:16 * t + 16]), 80,
-                [("vf", 0, 64)], [("vc", x, x + P)], lat=2200, sem=("d13" if t else "d12", 48 if t else 16))
-        if q > 0:
-            send(q, "v%d" % q, [(d, "vf", 16, 64, "vl", 48 * q) for d in range(q - 1, -1, -1)], cfg["rem"] + 1500)
-        vec(q, lambda g, T: g.vector.tensor_copy(T.enf[:], T.eni[:]), 32, [("eni", 0, 32)], [("enf", 0, 32)])
-        vec(q, lambda g, T: g.vector.transpose(T.ent[:], T.enf[:]), 32, [("enf", 0, 32)], [("ent", 0, 32)])
-        act(q, lambda g, T: g.scalar.activation(T.enm[:, 0:16], T.ent[:, 0:16], AF.Identity, scale=T.col[:, 12:13]), 16, [("ent", 0, 32), ("col", 12, 13)], [("enm", 0, 16)])
-        act(q, lambda g, T: g.scalar.activation(T.enm[:, 16:32], T.ent[:, 16:32], AF.Identity, scale=T.col[:, 8:9]), 16, [("ent", 0, 32), ("col", 8, 9)], [("enm", 16, 32)])
-        vec(q, lambda g, T: g.vector.tensor_tensor(T.es[:, W * q:W * q + W], T.enm[:, 0:16], T.enm[:, 16:32], A.add), 32, [("enm", 0, 32)], [("es", W * q, W * q + W)])
-        vec(q, lambda g, T: g.vector.tensor_scalar(T.bmt[0:64, :], T.bmc[0:64, :], 5, None, A.logical_shift_right), 512, [("bmc0", 0, 1)], [("bmt0", 0, 1)])
-        vec(q, lambda g, T: g.vector.tensor_scalar(T.bmt[64:128, :], T.bmc[64:128, :], 31, None, A.bitwise_and), 512, [("bmc1", 0, 1)], [("bmt1", 0, 1)])
-        half = [("colC", 0, 1), ("colD", 0, 1)]
-        fill(q, "col", slice(16, 17), 1, 1.0, half[0], slice(0, 64))
-        fill(q, "col", slice(16, 17), 1, 0.0, half[1], slice(64, 128))
-        act(q, lambda g, T: g.scalar.activation(T.col[:, 20:21], T.col[:, 16:17], AF.Identity, bias=16.0, scale=-16.0), 1, half, [("col", 20, 21)])
-        act(q, lambda g, T: g.scalar.activation(T.pb7[:, 0:512:2], T.cc[:], AF.Identity, scale=T.col[:, 16:17]), 256, half + [("cc", 0, 256)], [("pb7", 0, 1)])
-        act(q, lambda g, T: g.scalar.activation(T.pb7[:, 1:512:2], T.cc[:], AF.Identity, bias=T.col[:, 20:21], scale=T.col[:, 16:17]), 256,
-            half + [("cc", 0, 256), ("col", 20, 21)], [("pb7", 1, 2)])
-        vec(q, lambda g, T: g.vector.tensor_tensor(T.hl[:], T.bmt[:], T.pb7[:], A.add), 512,
-            [("bmt0", 0, 1), ("bmt1", 0, 1), ("pb7", 0, 512)], [("hl", 0, 512)])
-        for o in range(8):
-            b = "pb%d" % (3 + o % 4)
-            lo = 8 + 512 * o
-            c = 16.5 - 8192.0 * o - 65536.0 * q - LOW
-            pe(q, lambda g, T, o=o, b=b: g.tensor.matmul(T[b][:], T.sm[:, 128 * o:128 * o + 128], T.hl[:], True, True), 512,
-               [("sm", 128 * o, 128 * o + 128), ("hl", 0, 512)], [(b, 0, 512)])
-            if o % 2 == 0:
-                act(q, lambda g, T, b=b, lo=lo, c=c: g.scalar.activation(T.yt[:, lo:lo + 512], T[b][:], AF.Identity, bias=c), 512, [(b, 0, 512)], [("yt", lo, lo + 512)])
+            vec(q, "ts2", ap("sm", 128 * o, 128 * o + 128), ap("ibh", 0, 128), float(o), col(C_W), A.is_equal, A.mult)
+            ops[-1]["busy"] = cfg["fix"] + 64 * CYC
+        vec(q, "ts1", ap("j16", 0, 16), ap("i16", 0, 16), 15, A.bitwise_and)
+        vec(q, "ts2", ap("j1", 0, 1), ap("i16", 0, 1), 4, 1, A.logical_shift_right, A.bitwise_and)
+        vec(q, "cp", col(C_EVEN), ap("j1", 0, 1))
+        vec(q, "ts2", ap("da", 0, 16), ap("j16", 0, 16), 0.0, -BIG, A.is_equal, A.mult)
+        vec(q, "ts2", ap("db", 0, 16), ap("j16", 0, 16), 1.0, HUGE, A.is_equal, A.mult)
+        vec(q, "tt", ap("dd", z, z + 16), ap("da", 0, 16), ap("db", 0, 16), A.add)
+        for n in (16, 32, 64, 128):
+            act(q, ap("dd", z + n, z + 2 * n), ap("dd", z, z + n))
+        for h in range(q, NR - 1):
+            if h == q:
+                act(q, ap("dd", P * h, P * h + P), ap("dd", z, z + P))
             else:
-                vec(q, lambda g, T, b=b, lo=lo, c=c: g.vector.tensor_scalar(T.yt[:, lo:lo + 512], T[b][:], c, None, A.add), 512, [(b, 0, 512)], [("yt", lo, lo + 512)])
-        if cfg["cs"][q]:
-            for x in range(0, 512, 128):
-                fill(q, "zb", slice(x, x + 128), 128, 0.0, ("zb", x, x + 128))
-            for b in ("pb0", "pb1"):
-                if b == "pb0" or q < NR - 1:
-                    pe(q, lambda g, T, b=b: g.tensor.matmul(T[b][:], T.zb[:, 0:128], T.zb[:], True, False), 512, [("zb", 0, 512)], [(b, 0, 512)])
+                late.append((dma(q, "s", ap("dd", P * h, P * h + P), ap("dd", z, z + P), 2500), loaded))
+        act(q, col(C_ODD), col(C_EVEN), 1.0, -1.0)
+        act(q, col(C_K1), FIRST, 8 - 7.5 / 16 - 4096.0 * q, -1.0 / 16)
+        act(q, col(C_T), FIN, 8 + 16.5 / 32 + BIG / 32, 1.0 / 32)
+        act(q, col(C_K2), FIRST, col(C_T), -1.0 / 32)
+        if q < NR - 1:
+            act(q, col(C_TOP), FIRST, 65536.0 * (q + 1))
+        act(q, col(C_S1), FIN, None, CAP / BIG)
+        act(q, col(C_S2), FIN, -CAP, -CAP / BIG)
+        act(q, col(C_WC), FIN, -CAP, -16 * CAP / BIG)
+        if q:
+            act(q, col(C_END), FIN, 5 * LESS, 4 * q * 2 * MID / BIG)
+        vec(q, "cp", ap("g8h", 0, 128, 1, EIGHT), ap("g8", 0, 128, 1, EIGHT))
+        act(q, ap("r2", 0, 128), ap("rr", 0, 128), col(C_S2), col(C_S1))
+        call(q, "a", "sign", (ap("r3", 0, 128), ap("rr", 0, 128)), 180)
+        act(q, ap("r4", 0, 128), ap("r3", 0, 128), col(C_WC), FIN)
+        fill(q, ap("r1", 0, 128), -1.0)
+        blocks("wk", "t2", ap("r2", 0, 128))
+        blocks("wc", "t4", ap("r4", 0, 128))
+        blocks("wy", "t1", ap("r1", 0, 128))
+        act(q, ap("idb", 0, 128), ap("idn", 0, 128))
+        fill(q, ap("yt", 0, 8), -OUT)
+        fill(q, ap("yt", 4104, 4112), -OUT if q else -16.0)
+        for x in (0, 2056):
+            vec(q, "ts2", ap("csi", x, x + 8), ap("ones", 0, 8), FIN, -2 * MID / BIG, A.mult, A.mult)
+            fill(q, ap("lsb", x, x + 8), 0.0)
+        if CAST and floats(q):
+            dma(q, "g", CSF, CSI, cfg["t_cast"])
+            ops[-1]["busy"] = cfg["t_g"]
+        for t in range(4):
+            i = vec(q, "ts2", ap("vi", t, 64, 4), ap("sdi", 0, 16), 4 * t, 4095, A.logical_shift_right, A.bitwise_and)
+            ops[i]["deps"] = {j for j in ops[i]["deps"] if ops[j]["name"] != "vi"}
+        vec(q, "ts1", ap("vf", 0, 64), ap("vi", 0, 64), -MID, A.add)
+        dma(q, "s", ap("vc", 4 * P * q, 4 * P * (q + 1), 1, EIGHT), ap("vf", 0, 64), 2200)
+        if q > 0:
+            i = send(q, [(d, ap("vf", 0, 64), ap("vd%d" % q, 0, 64)) for d in range(q - 1, -1, -1)])
+            ops[i]["deps"].add(max(j for j in range(begin, i) if ops[j]["kind"] == "sel"))
+        vec(q, "cp", ap("enf", 0, 32), ap("eni", 0, 32))
+        vec(q, "tr", ap("ent", 0, 32), ap("enf", 0, 32))
+        act(q, ap("enm", 0, 16), ap("ent", 0, 16), FIRST, col(C_EVEN))
+        act(q, ap("enm", 16, 32), ap("ent", 16, 32), 0.0, col(C_ODD))
+        vec(q, "tt", last("dd", P * q, P * q + P), ap("enm", 0, 16), ap("enm", 16, 32), A.add)
+        act(q, ap("pb7", 0, 512, 2), ap("cc", 0, 256), 0.0, col(C_LOW))
+        act(q, ap("pb7", 1, 512, 2), ap("cc", 0, 256), col(C_16), col(C_LOW))
+        vec(q, "ts1", ap("bmt", 0, 512, 1, LO), ap("bmc", 0, 512, 1, LO), 5, A.logical_shift_right)
+        vec(q, "ts1", ap("bmt", 0, 512, 1, HI), ap("bmc", 0, 512, 1, LO if cfg["once"] else HI), 31, A.bitwise_and)
+        vec(q, "tt", ap("hl", 0, 512), ap("bmt", 0, 512), ap("pb7", 0, 512), A.add)
+        for o in range(8):
+            b, lo, c = ap("pb%d" % (2 + o % 5), 0, 512), 8 + 512 * o, -8192.0 * o - 65536.0 * q
+            mm(q, b, ap("sm", 128 * o, 128 * o + 128), ap("hl", 0, 512), True, True)
+            if cfg["evac"][q][o] == "a":
+                act(q, ap("yt", lo, lo + 512), b, c)
+            else:
+                built = vec(q, "ts1", ap("yt", lo, lo + 512), b, c, A.add)
+        for i in range(begin, built if q else 0):
+            if ops[i]["e"] == "v" and ops[i]["name"] == "csi":
+                late.append((i, built))
+        for b in sorted({sum_at(q, P * h, P * h)[0] for h in range(q, NR)}):
+            mm(q, ap(b, 0, 512), ap("zb", 0, 128), ap("lsb", 8, 520), True, False)
+        if not CAST and floats(q):
             for x in range(0, 2048, 512):
-                hi = x + 512 + (8 if x == 1536 else 0)
-                vec(q, lambda g, T, x=x, hi=hi: g.vector.tensor_scalar(T.csf[:, x:hi], T.csi[:, x:hi], -MID, None, A.add), 512, [("csi", x, hi)], [("csf", x, hi)])
+                hi = x + 512 + (16 if x == 1536 else 0)
+                vec(q, "ts1", ap("csf", x, hi), ap("csi", x, hi), -MID, A.add)
 
     def visitors_v(q):
-        for k, h in enumerate(range(q + 1, NR)):
-            for t in range(1, 4):
-                x = vpos[(q, h, t)]
-                add(q, "s", lambda g, T, h=h, t=t, x=x: g.sync.dma_start(T.vc[0:8, x:x + P], T.vl[:, 48 * h + 16 * t - 16:48 * h + 16 * t]), 80,
-                    [("vl", 48 * h, 48 * h + 48)], [("vc", x, x + P)], lat=2300, sem=("d%d" % (9 + k), 48))
+        for h in range(NR - 1, q, -1):
+            dma(q, "s", ap("vc", 4 * P * h, 4 * P * (h + 1), 1, EIGHT), ap("vd%d" % h, 0, 64), 2000)
 
-    def tally_at(q, h):
-        if not cfg["cs"][q]:
-            return "tl", P * h
-        if q == 0:
-            return "pb%d" % (h // 2), P * (h % 2)
-        return ("pb0", 0) if h == q else ("pb1", P * (h - q - 1))
+    def zero_bin():
+        at = ap("oz", 0, 1)
+        vec(0, "ts2", at, ap("yt", 8, 9), 1.0 / 32, 8 + 16.5 / 32, A.mult, A.add)
+        gather(0, "a", ap("zi", 0, 16), CSF, at)
+        act(0, ap("csf", 0, 8), ap("zi", 0, 8))
+        vec(0, "ts1", ap("csi", 0, 8), ap("zi", 0, 8), LESS, A.add)
+        gather(0, "a", ap("zl", 0, 16), LS, at)
+        act(0, ap("lsb", 0, 8), ap("zl", 0, 8))
 
-    def give_back(q, part, h0, h1):
+    def chunks(lo, hi):
+        return [(h, max(lo, P * h), min(hi, P * h + P)) for h in range((hi - 1) // P, lo // P - 1, -1)]
+
+    def sum_at(q, lo, hi):
+        h = lo // P
+        b, x = ("pb0", 0) if h == q else ("pb1", P * (h - 2)) if h >= 2 else ("pb%d" % cfg["one"], P)
+        return ap(b, x + lo - P * h, x + hi - P * h)
+
+    def tally(q, lo, hi, src):
+        i = mm(q, sum_at(q, lo, hi), ap("idn", 0, 128), src, False, False)
+        ops[i]["sum"] = ops[i]["name"]
+
+    back = {h: [] for h in range(NR)}
+
+    def give_back(q, part, lo, hi):
+        cut = chunks(lo, hi)
         least = min(len(topo.engines(cores[q], cores[x])) for x in range(q + 1, NR))
-        same = [h for h in range(h0, h1) if len(topo.engines(cores[q], cores[h])) > least]
-        far = [x for x in range(q + 1, NR) if x not in same] if len(same) == h1 - h0 else []
-        send(q, "f%d%d" % (q, part), [(h, "tu", 1024 * part + P * h, 1024 * part + P * h + P, "tin", P * (2 * q + part)) for h in range(h1 - 1, h0 - 1, -1)],
-             cfg["rem"] + 500 * (h1 - h0), far)
+        same = [h for h, _, _ in cut if len(topo.engines(cores[q], cores[h])) > least]
+        far = [x for x in range(q + 1, NR) if x not in same] if len(same) == len(cut) else []
+        items = []
+        for h, a, b in cut:
+            x = P * (2 * q + part - h)
+            items.append((h, ap("tu", 1024 * part + a, 1024 * part + b), ap("tin", x + a, x + b)))
+            back[h].append((part, q, a - P * h, b - P * h))
+        send(q, items, far if cfg["leave"] else ())
 
-    nv = [0] * NR
+    def state(q, t, lo, hi):
+        return wrapped("es", t, lo, hi) if q else last("dd", lo, hi)
 
-    def task(q, r, st, h0, h1, h2):
-        n, w = P * (h1 - h0), W * (h1 - h0)
-        z = P * h0
-        c0 = 64 * r + W * h0
-        CS = ("csi", 0, 2056)
-        if r == 2 and max(h0, q + 1) < h1:
-            l0, l1 = W * max(h0, q + 1), W * h1
-            vec(q, lambda g, T: g.vector.tensor_scalar(T.es[:, 128 + l0:128 + l1], T.land[:, l0:l1], 65536.0 * (q + 1), None, A.min),
-                l1 - l0, [("land", l0, l1)], [("es", 128 + l0, 128 + l1)])
-        E, O1, O2 = ("es", c0, c0 + w), ("o1", c0, c0 + w), ("o2", c0, c0 + w)
-        shift = -7.5 / 16 + (8.0 - 4096.0 * q if q else 0.0)
-        y0 = 0 if q else 8
-        vec(q, lambda g, T: g.vector.tensor_scalar(T.o1[:, c0:c0 + w], T.es[:, c0:c0 + w], 1.0 / 16, shift, A.mult, A.add), w, [E], [O1])
-        act(q, lambda g, T: g.scalar.activation(T.d0[:, z:z + n:16], T.es[:, c0:c0 + w], AF.Identity if q else AF.Relu), w, [E], [("d0", z, z + n)])
-        vec(q, lambda g, T: g.vector.tensor_tensor(T.xx[:, z:z + n], T.yt[:, y0:4112].indirect(T.o1[:, c0:c0 + w]), T.wm[:, 0:n], A.mult), GAT * n,
-            [("yt", 0, 4112), O1, ("wm", 0, n)], [("xx", z, z + n)])
-        vec(q, lambda g, T: g.vector.tensor_tensor_scan(T.yy[:, z:z + n], T.d0[:, z:z + n], T.xx[:, z:z + n], -LOW, A.max, A.add), n,
-            [("d0", z, z + n), ("xx", z, z + n)], [("yy", z, z + n)])
-        vec(q, lambda g, T: g.vector.tensor_scalar(T.o2[:, c0:c0 + w], T.yy[:, z + 15:z + n:16], 1.0 / 32, LOW / 32 + 8, A.mult, A.add), w,
-            [("yy", z, z + n)], [O2])
-        if r == 5:
-            for h in range(h1 - 1, h0 - 1, -1):
-                c, x = 64 * r + W * h, 1024 + P * h
-                vec(q, lambda g, T, c=c, x=x: g.vector.tensor_copy(T.tu[:, x:x + P], T.csi[:, 0:2056].indirect(T.o2[:, c:c + W])), GAT * P,
-                    [CS, ("o2", c, c + W)], [("tu", x, x + P)])
-                give_back(q, 1, h, h + 1)
+    def task(q, t, lo, hi, ba, bb, on):
+        n, own = hi - lo, lo // P == q
+        if t == 1 and not own:
+            vec(q, "ts1", state(q, 1, lo, hi), wrapped("land", 0, lo, hi), col(C_TOP), A.min)
+        DD, XX, Y1, Y2 = ap("dd", lo, hi), ap("xx", lo, hi), ap("y1", lo, hi), ap("y2", lo, hi)
+        E = state(q, t, lo, hi) if not own else last("y2", lo, hi) if t else last("dd", lo, hi)
+        O1, O2 = wrapped("o1", t, lo, hi), wrapped("o2", t, lo, hi)
+        vec(q, "ts2", O1, E, 1.0 / 16, col(C_K1), A.mult, A.add)
+        if E[0] != "dd":
+            (vec(q, "cp", last("dd", lo, hi), E) if on[3] == "v" else act(q, last("dd", lo, hi), E))
+        gather(q, on[0], XX, ap("yt", 0, 4112), O1)
+        vec(q, "scan", Y1, XX, DD)
+        vec(q, "ts2", O2, last("y1", lo, hi), 1.0 / 32, col(C_K2), A.mult, A.add)
+        zc = 1024 * (t % 2)
+        fused = on[1] in "fF" and t < 4
+        cs_on = "v" if t == 0 or on[1] in "vF" else "a"
+
+        def sections(a, b):
+            gather(q, cs_on, ap("cg", zc + a, zc + b), CSF if cs_on == "a" else CSI, wrapped("o2", t, a, b), -LESS)
+        if t == 4 and not own:
+            for h, a, b in chunks(lo, hi):
+                if h in cfg["whole"][q]:
+                    sections(a, b)
+                    tally(q, a, b, ap("cg", zc + a, zc + b))
+                else:
+                    gather(q, "v", ap("tu", 1024 + a, 1024 + b), CSI, wrapped("o2", t, a, b))
+                    give_back(q, 1, a, b)
             return
-        zc = z + 1024 * (r % 2)
-        if cfg["cs"][q]:
-            act(q, lambda g, T: g.scalar.activation(T.cg[:, zc:zc + n], T.csf[:, 0:2056].indirect(T.o2[:, c0:c0 + w]), AF.Copy), GAT * n,
-                [("csf", 0, 2056), O2], [("cg", zc, zc + n)])
-        if h2 < h1:
-            m, u = P * (h1 - h2), W * (h1 - h2)
-            c2, z2 = 64 * r + W * h2, zc + P * (h2 - h0)
-            S2, LS, CM, SE = ("o2", c2, c2 + u), ("lsb", 0, 2056), ("cmpb", z, z + m), ("selb", z, z + m)
-            x = vpos[(q, h2, event_of(q, h2, r))]
-            bv, bk = vbanks(q)[nv[q] % len(vbanks(q))], "pb%d" % (3 + st)
-            nv[q] += 1
-            pe(q, lambda g, T: g.tensor.matmul(T[bv][:, 0:m], T.g8h[0:8, :], T.vc[0:8, x:x + m], True, True), m, [("g8h", 0, 128), ("vc", x, x + m)], [(bv, 0, m)])
-            if cfg["cs"][q]:
-                vec(q, lambda g, T: g.vector.tensor_tensor(T.cmpb[:, z:z + m], T.cg[:, z2:z2 + m], T[bv][:, 0:m], A.is_le), m, [("cg", z2, z2 + m), (bv, 0, m)], [CM])
+        if not fused:
+            sections(lo, hi)
+        if t < 4:
+            LG, CM, YB = ap("lg", lo, hi), ap("cmpb", lo, hi), ap("yb", lo, hi)
+            PA, PX = ap("pb%d" % ba, 0, n), ap("pb%d" % bb, P * (ba == bb), P * (ba == bb) + n)
+            mm(q, PA, ap("g8h", 0, 128, 1, EIGHT), ap("vc", 4 * lo + t, 4 * hi, 4, EIGHT), True, fused or not CAST)
+            if fused:
+                act(q, ap("vb", lo, hi), PA, MID)
+                vec(q, "tt", CM, ind(CSI, O2), ap("vb", lo, hi), A.is_gt)
             else:
-                act(q, lambda g, T: g.scalar.activation(T.vb[:, x:x + m], T[bv][:, 0:m], AF.Identity, bias=MID), m, [(bv, 0, m)], [("vb", x, x + m)])
-                vec(q, lambda g, T: g.vector.tensor_tensor(T.cmpb[:, z:z + m], T.csi[:, 0:2056].indirect(T.o2[:, c2:c2 + u]), T.vb[:, x:x + m], A.is_le), GAT * m,
-                    [CS, S2, ("vb", x, x + m)], [CM])
-            pe(q, lambda g, T: g.tensor.matmul(T[bk][:, 0:m], T.fb[:], T.cmpb[:, z:z + m], True, True), m, [("fb", 0, 128), CM], [(bk, 0, m)])
-            mb, m0 = (bk, 0) if cfg["ls"][q] else ("msk", z)
-            if cfg["mask"][q]:
-                act(q, lambda g, T: g.scalar.activation(T.ab[:, z:z + m], T[bk][:, 0:m], AF.Abs, bias=T.col[:, 4:5]), m, [(bk, 0, m), ("col", 4, 5)], [("ab", z, z + m)])
-                act(q, lambda g, T: g.scalar.activation(T[mb][:, m0:m0 + m], T.ab[:, z:z + m], AF.Relu, bias=1.0, scale=-1.0), m, [("ab", z, z + m)], [(mb, m0, m0 + m)])
-            else:
-                vec(q, lambda g, T: g.vector.tensor_scalar(T[mb][:, m0:m0 + m], T[bk][:, 0:m], T.col[:, 4:5], None, A.is_equal), m, [(bk, 0, m), ("col", 4, 5)], [(mb, m0, m0 + m)])
-            if cfg["ls"][q]:
-                act(q, lambda g, T: g.scalar.activation(T.lg[:, z:z + m], T.lsb[:, 0:2056].indirect(T.o2[:, c2:c2 + u]), AF.Copy), GAT * m, [LS, S2], [("lg", z, z + m)])
-                vec(q, lambda g, T: g.vector.tensor_tensor(T.selb[:, z:z + m], T.lg[:, z:z + m], T[bk][:, 0:m], A.mult), m, [("lg", z, z + m), (bk, 0, m)], [SE])
-            else:
-                vec(q, lambda g, T: g.vector.tensor_tensor(T.selb[:, z:z + m], T.lsb[:, 0:2056].indirect(T.o2[:, c2:c2 + u]), T.msk[:, z:z + m], A.mult), GAT * m,
-                    [LS, S2, ("msk", z, z + m)], [SE])
-            pe(q, lambda g, T: g.tensor.matmul(T[bk][:, 0:u], T.idn[:], T.es[:, c2:c2 + u], True, False), 256, [("idn", 0, 128), ("es", c2, c2 + u)], [(bk, 0, u)])
-
-            def wrap(g, T):
-                for i in range(16):
-                    last = g.tensor.matmul(T[bk][:, 0:u], T.hm[:, 16 - i:144 - i], T.selb[:, z + i:z + m:16], False, i == 15)
-                return last
-            pe(q, wrap, 1024, [("hm", 0, 144), SE], [(bk, 0, u)])
-            a, nx = h2, c2 + 64
-            if h2 == q:
-                act(q, lambda g, T: g.scalar.activation(T.es[:, nx:nx + W], T[bk][:, 0:W], AF.Copy), W, [(bk, 0, W)], [("es", nx, nx + W)])
-                a += 1
+                if CAST:
+                    mm(q, PA, ap("mid", 0, 128, 1, (0, 1)), ap("onb", 0, n, 1, (0, 1)), False, True)
+                vec(q, "tt", CM, ap("cg", zc + lo, zc + hi), PA, A.is_gt)
+            gather(q, on[2], LG, LS, O2)
+            mm(q, PX, ap("wk", 0, 128), CM, True, False)
+            pick = mm(q, PX, ap("idb", 0, 128), LG, False, True)
+            if ba != bb:
+                ops[mm(q, PA, ap("wc", 0, 128), CM, True, False)]["deps"].add(pick)
+            vec(q, "ts2", YB, PX, 0.0, CAP, A.max, A.min)
+            if ba == bb:
+                mm(q, PA, ap("wc", 0, 128), CM, True, False)
+            pick = mm(q, PA, ap("wy", 0, 128), YB, False, True)
+            vec(q, "scan", Y2, PA, DD)
+            NEW, ES, LAND = last("y2", lo, hi), state(q, t + 1, lo, hi), wrapped("land", t, lo, hi)
+            lower = list(range(q - 1, -1, -1))
+            direct = cfg["direct"] and t == 1 and lo >= P * (NR - 1) and not own
+            if own:
                 if q > 0:
-                    send(q, "r%d0%d" % (q, r), [(d, "es", nx, nx + W, "land", 64 * r + W * q) for d in (range(q - 1, -1, -1) if r == 0 else [q - 1])], cfg["rem"])
-            if a < h1:
-                t, lo, hi, e0 = r - 1, W * a, W * h1, 64 * r + 64
-                vec(q, lambda g, T: g.vector.tensor_tensor(T.es[:, e0 + lo:e0 + hi], T.land[:, 64 * t + lo:64 * t + hi], T[bk][:, lo - W * h2:hi - W * h2], A.min),
-                    hi - lo, [("land", 64 * t + lo, 64 * t + hi), (bk, 0, u)], [("es", e0 + lo, e0 + hi)])
+                    act(q, ES, NEW)
+                    if t or cfg["apart"]:
+                        send(q, [(q - 1, ES, LAND)])
+                    if t == 0 and lower[cfg["apart"]:]:
+                        send(q, [(d, ES, LAND) for d in lower[cfg["apart"]:]])
+            elif direct and q < NR - 2:
+                mine = wrapped("mine", 0, lo, hi)
                 if q > 0:
-                    send(q, "r%d%d%d" % (q, st, t), [(q - 1, "es", e0 + lo, e0 + hi, "land", 64 * t + lo)], cfg["rem"])
-        b, x0 = tally_at(q, h0)
-        if cfg["cs"][q]:
-            for k in range(0, n, cfg["tw"]):
-                me, e = len(ops), k + cfg["tw"]
-                pe(q, lambda g, T, me=me, k=k, e=e: g.tensor.matmul(T[b][:, x0 + k:x0 + e], T.idn[:], T.cg[:, zc + k:zc + e], False, closing[(q, b)] == me), 4 * (e - k),
-                   [("idn", 0, 128), ("cg", zc + k, zc + e)], [(b, x0 + k, x0 + e)])
-                ops[me]["sum"] = b
-        elif r == (0 if h0 == q else 2):
-            vec(q, lambda g, T: g.vector.tensor_copy(T.tl[:, x0:x0 + n], T.csi[:, 0:2056].indirect(T.o2[:, c0:c0 + w])), GAT * n, [CS, O2], [("tl", x0, x0 + n)])
-        else:
-            vec(q, lambda g, T: g.vector.tensor_tensor(T.tl[:, x0:x0 + n], T.csi[:, 0:2056].indirect(T.o2[:, c0:c0 + w]), T.tl[:, x0:x0 + n], A.add), GAT * n,
-                [CS, O2, ("tl", x0, x0 + n)], [("tl", x0, x0 + n)])
+                    act(q, mine, NEW)
+                    send(q, [(d, mine, wrapped("more", q, lo, hi)) for d in lower])
+                for s in range(q + 1, NR - 2):
+                    vec(q, "tt", mine, wrapped("more", s, lo, hi), NEW, A.min)
+                    NEW = mine
+                vec(q, "tt", ES, LAND, NEW, A.min)
+            else:
+                vec(q, "tt", ES, LAND, NEW, A.min)
+                if q > 0:
+                    send(q, [(d, ES, LAND) for d in (lower if direct else lower[:1])])
+            if fused:
+                sections(lo, hi)
+        for h, a, b in chunks(lo, hi):
+            if t == 1 and h in cfg["early"][q]:
+                vec(q, "ts1", ap("tu", a, b), ap("cg", zc + a, zc + b), LESS, A.add)
+                give_back(q, 0, a, b)
+                continue
+            tally(q, a, b, ap("cg", zc + a, zc + b))
+            if t < 4:
+                ops[-1]["deps"].add(pick)
 
-    def partial(q):
-        for (a, b) in ((1, 2), (2, NR)) if q == 0 else ((q + 1, NR),):
-            bf, x = tally_at(q, a)
-            n = P * (b - a)
-            vec(q, lambda g, T, a=a, b=b, bf=bf, x=x, n=n: g.vector.tensor_scalar(T.tu[:, P * a:P * b], T[bf][:, x:x + n], 3 * MID * cfg["cs"][q], None, A.add),
-                n, [(bf, x, x + n)], [("tu", P * a, P * b)])
-            give_back(q, 0, a, b)
+    def sums(q, whole):
+        hs = [h for h in range(q + 1, NR) if (h in cfg["whole"][q]) == whole]
+        for run in ([h for h in hs if h >= 2], [h for h in hs if h < 2]):
+            if run:
+                a, e = P * run[0], P * run[-1] + P
+                b, x = sum_at(q, a, a)[:2]
+                part = int(run[0] in cfg["early"][q])
+                vec(q, "ts1", ap("tu", 1024 * part + a, 1024 * part + e), ap(b, x, x + e - a), (4 - part if whole else 3) * LESS, A.add)
+                give_back(q, part, a, e)
 
     def finish(q):
-        b, x = tally_at(q, q)
-        if cfg["cs"][q]:
-            act(q, lambda g, T, b=b, x=x: g.scalar.activation(T.acc[:, 0:P], T[b][:, x:x + P], AF.Identity, bias=5 * MID), P, [(b, x, x + P)], [("acc", 0, P)])
-            b, x = "acc", 0
-        k = 0
-        for part in range(2):
-            for s in range(q - 1, -1, -1):
-                pb, i0 = "pb%d" % (6 + k % 2), P * (2 * s + part)
-                k += 1
-                o = P * k
-                vec(q, lambda g, T, i0=i0, pb=pb: g.vector.tensor_copy(T[pb][:, 0:P], T.tin[:, i0:i0 + P]), P, [("tin", i0, i0 + P)], [(pb, 0, P)])
-                vec(q, lambda g, T, b=b, x=x, pb=pb, o=o: g.vector.tensor_tensor(T.acc[:, o:o + P], T[b][:, x:x + P], T[pb][:, 0:P], A.add), P,
-                    [(b, x, x + P), (pb, 0, P)], [("acc", o, o + P)])
-                b, x = "acc", o
-        dma(q, "s", lambda g, T: g.sync.dma_start(T.y[:], T[b][:, x:x + P]), 2500, [(b, x, x + P)], [("y", 0, 1)])
+        OWN, ACC = ap("pb0", 0, P), ap("acc", 0, P)
+        for part, s, a, b in sorted(back[q]):
+            if s > 0:
+                x = P * (2 * s + part)
+                vec(q, "cp", ap("tf", x + a, x + b), ap("tin", x + a, x + b))
+                tally(q, P * q + a, P * q + b, ap("tf", x + a, x + b))
+        if q:
+            vec(q, "ts1", ap("tf", 0, P), ap("tin", 0, P), col(C_END), A.add)
+            vec(q, "tt", ACC, OWN, ap("tf", 0, P), A.add)
+        else:
+            act(q, ACC, OWN, 5 * LESS)
+        ends = [(a, b) for part, s, a, b in back[q] if s == 0 and part == 1]
+        for a, b in ends:
+            vec(q, "cp", ap("pb7", a, b), ap("tin", P + a, P + b))
+            vec(q, "tt", ap("acc", P + a, P + b), ap("acc", a, b), ap("pb7", a, b), A.add)
+            dma(q, "s", ap("y", a, b), ap("acc", P + a, P + b), 1500 + 2 * (b - a))
+        if not ends:
+            dma(q, "s", ap("y", 0, P), ACC, 2000)
 
     for q in range(NR):
         start(q)
     for rnd in range(6):
         for q in range(NR - 1, -1, -1):
-            if rnd == 5 and q < NR - 1:
-                partial(q)
-            for tk in TASKS[q]:
-                if tk[0] == rnd:
-                    tag[0] = "%d%d%d" % (q, tk[0], tk[1])
-                    task(q, *tk)
+            if rnd == 5:
+                sums(q, False)
+            for k, s in reversed(list(enumerate(cfg["streams"][q]))):
+                t = rnd if s[0] // P == q else rnd - 1
+                if t <= 4 and (t > 0 or t == rnd):
+                    tag[0] = "%d%d%d" % (q, rnd, k)
+                    task(q, t, *s)
                     tag[0] = None
             if rnd == 0:
                 visitors_v(q)
+                if q == 0:
+                    zero_bin()
+            if rnd == 5:
+                sums(q, True)
     for q in range(NR):
         finish(q)
-
-    share = {}
-    for i, o in enumerate(ops):
-        if o["sem"]:
-            share.setdefault((o["q"], o["sem"][0]), []).append(i)
-    for o in ops:
-        for j in list(o["deps"]):
-            if ops[j]["sem"]:
-                o["deps"].update(share[(ops[j]["q"], ops[j]["sem"][0])])
 
     n = len(ops)
     users = [[] for _ in range(n)]
@@ -404,34 +484,59 @@ def build(cores, topo, cfg):
     tail = [0.0] * n
     for i in range(n - 1, -1, -1):
         tail[i] = ops[i]["busy"] + ops[i]["lat"] + max([tail[u] + HOP for u in users[i]] + [0.0])
-    seed = cfg["seed"]
-    for i in range(n):
-        seed = (seed * 1103515245 + 12345) % 2147483648
-        tail[i] += cfg["prio"].get(ops[i]["tag"], 0.0) + ops[i].get("boost", 0.0) + cfg["noise"] * seed / 2147483648
-    left = [len(o["deps"]) for o in ops]
-    ready = [i for i in range(n) if left[i] == 0]
-    can, free, order, end = [0.0] * n, {}, [], 0.0
-    while ready:
-        st = {i: max(can[i], free.get((ops[i]["q"], ops[i]["e"]), 0.0)) for i in ready}
-        i0 = min(ready, key=lambda i: (st[i], i))
-        key = (ops[i0]["q"], ops[i0]["e"])
-        near = [i for i in ready if (ops[i]["q"], ops[i]["e"]) == key and st[i] <= st[i0] + min(cfg["look"], cfg["lk2"] * ops[i0]["busy"])
-                and (i == i0 or tail[i] > tail[i0] + cfg["marg"])]
-        i = max(near, key=lambda i: (tail[i], -i))
-        ready.remove(i)
-        o = ops[i]
-        o["t"] = st[i]
-        free[key] = st[i] + o["busy"]
-        done = free[key] + o["lat"]
-        end = max(end, done)
-        order.append(i)
-        for u in users[i]:
-            same = o["e"] == ops[u]["e"] and o["q"] == ops[u]["q"] and o["e"] == "p"
-            can[u] = max(can[u], done + (0.0 if same else HOP))
-            left[u] -= 1
-            if left[u] == 0:
-                ready.append(u)
-    count = {}
+    for i, j in late:
+        ops[i]["deps"].add(j)
+        users[j].append(i)
+    queue = [5 * o["q"] + "vapgs".index(o["e"]) for o in ops]
+    gap = [[(u, 0.0 if queue[u] == queue[i] and o["e"] == "p" else (o["lats"][ops[u]["q"]] if o["rem"] else o["lat"]) + HOP)
+            for u in users[i]] for i, o in enumerate(ops)]
+    NEVER = 1e18
+
+    def schedule(prio):
+        rank = [tail[i] + prio.get(o["tag"], 0.0) + o.get("boost", 0.0) - 1e-3 * i for i, o in enumerate(ops)]
+        left, can, at, end = [len(o["deps"]) for o in ops], [0.0] * n, [0.0] * n, 0.0
+        ready, free, used = [[] for _ in range(5 * NR)], [0.0] * (5 * NR), [set() for _ in range(NR)]
+        for i in range(n):
+            if not left[i]:
+                ready[queue[i]].append(i)
+        soon = [0.0 if r else NEVER for r in ready]
+        for _ in range(n):
+            t, k = min((max(a, b), k) for k, (a, b) in enumerate(zip(soon, free)))
+            i = max((i for i in ready[k] if can[i] <= t + cfg["look"][k // 5]), key=lambda i: rank[i])
+            ready[k].remove(i)
+            at[i] = max(t, can[i])
+            e = at[i] + ops[i]["busy"]
+            if ops[i]["rem"]:
+                e += (0.0 if used[k // 5] else cfg["first"]) + cfg["fresh"] * len(ops[i]["uses"] - used[k // 5])
+                used[k // 5] |= ops[i]["uses"]
+            free[k] = e
+            end = max(end, e + ops[i]["lat"])
+            soon[k] = min([can[j] for j in ready[k]] + [NEVER])
+            for u, d in gap[i]:
+                can[u] = max(can[u], e + d)
+                left[u] -= 1
+                if not left[u]:
+                    ready[queue[u]].append(u)
+                    soon[queue[u]] = min(soon[queue[u]], can[u])
+        return end, at
+
+    tags, seed, prio = sorted({o["tag"] for o in ops if o["tag"]}), cfg["seed"], dict(cfg["prio"])
+    now = best = schedule(prio)
+    for step in range(cfg["tries"]):
+        trial = dict(prio)
+        for _ in range(2):
+            seed = (seed * 1103515245 + 12345) % 2147483648
+            tg = tags[(seed >> 8) % len(tags)]
+            trial[tg] = trial.get(tg, 0.0) + (-3000, -1500, -500, 500, 1500, 3000)[(seed >> 20) % 6]
+        res = schedule(trial)
+        if res[0] <= now[0] + cfg["slack"] * (1 - step / cfg["tries"]):
+            prio, now = trial, res
+            best = min(best, res, key=lambda x: x[0])
+    end, at = best
+    for i, o in enumerate(ops):
+        o["t"] = at[i]
+    order = sorted(range(n), key=lambda i: (at[i], i))
+    count, closing = {}, {}
     for i in order:
         o = ops[i]
         if "sum" in o:
@@ -442,7 +547,19 @@ def build(cores, topo, cfg):
             key = (o["q"], o["e"])
             count[key] = count.get(key, 0) + 1
             o["sig"] = (COUNT[o["e"]], count[key])
+    for i in closing.values():
+        ops[i]["args"][4] = True
     return ops, order, end
+
+
+def emit(g, T, o, topo):
+    if o["kind"] != "send":
+        return CALLS[o["kind"]](g, *[real(T, a) for a in o["args"]])
+    src, tr = o["args"][0], []
+    for core, mask, sem, a, b in o["args"][1]:
+        rid, pid = topo.addr(core, src)
+        tr.append(RemoteDMATransfer(dst_ids=[DstId(rid=rid, pnc=pid)], dma_engine_mask=mask, remote_sem=T.sem[sem], src=real(T, a), dst=real(T, b)))
+    return g.remote_dma_fused(tr, local_sem=T.sem.sent)
 
 
 PLAN = {}
@@ -459,18 +576,18 @@ def rank_program(g, core, T, topo):
     seen, total = {}, {}
     for i in order:
         o = ops[i]
-        if o["rem"] and q in o["rem"][1]:
-            total[o["rem"][0]] = total.get(o["rem"][0], 0) + o["rem"][1][q]
+        if o["rem"] and q in o["rem"]:
+            total[o["rem"][q][0]] = o["rem"][q][1]
         if o["q"] != q:
             continue
         need = {}
         for j in o["deps"]:
             d = ops[j]
             if d["rem"]:
-                s, v = d["rem"][0], d["rem"][1][q]
+                s, v = d["rem"][q]
             elif d["e"] == "p" and o["e"] == "p":
                 continue
-            elif d["e"] == "g" and o["e"] == "g" and d["w"][0] != "f0":
+            elif d["e"] == "g" and o["e"] == "g" and (o["rem"] or d["args"][0] not in o["args"]):
                 continue
             else:
                 s, v = d["sig"]
@@ -479,9 +596,9 @@ def rank_program(g, core, T, topo):
             if seen.get((o["e"], s), 0) < v:
                 seen[(o["e"], s)] = v
                 queue[o["e"]].wait_ge(T.sem[s], v)
-        r = o["fn"](g, T)
+        r = emit(g, T, o, topo)
         if o["rem"]:
-            total["sent"] = total.get("sent", 0) + sum(o["rem"][1].values())
+            total["sent"] = total.get("sent", 0) + sum(v for _, v in o["rem"].values())
         else:
             r.then_inc(T.sem[o["sig"][0]], 16 if o["sem"] else 1)
             total[o["sig"][0]] = o["sig"][1]

@@ -4,17 +4,31 @@ from concourse.mybir import AluOpType as A, ActivationFunctionType as AF
 NR, P, W = 4, 256, 16
 BIG, HUGE, OUT, CAP, MID = float(1 << 20), float(1 << 22), float(1 << 19), float(1 << 18), 2048.0
 CFG = {
-    "streams": (((0, 256, 2, 2, "aaaa"), (256, 512, 3, 3, "aaaa"), (512, 768, 4, 4, "aaaa"), (768, 1024, 5, 6, "aaaa")),
-                ((256, 512, 2, 3, "aaaa"), (512, 768, 4, 5, "aaaa"), (768, 1024, 6, 7, "aaav")),
-                ((512, 768, 2, 3, "avav"), (768, 1024, 4, 5, "avav")),
-                ((768, 1024, 2, 3, "avav"),)),
-    "direct": True, "evac": ("aavaaaav", "avavavav", "avavavav", "avavavav"), "cast": False, "once": False,
-    "apart": 0, "leave": False, "one": 7,
-    "whole": ((1,), (), (), ()), "early": ((1,), (), (), ()),
-    "fix": 50.0, "pfix": 10.0, "cyc": 0.88, "gat": 1.56, "hop": 100.0, "pe": 0.45, "rem": 1200.0, "row": 50.0, "byte": 0.06,
-    "issue": 500.0, "first": 1500.0, "fresh": 100.0, "t_in": 2000.0, "t_cs": 5800.0,
-    "t_ls": 7200.0, "t_g": 1000.0, "t_cast": 4000.0, "look": (60.0, 60.0, 60.0, 60.0), "prio": {}, "seed": 1, "tries": 500, "slack": 200.0,
+    "streams": (((0, 256, 2, 2, "afaa"), (256, 512, 3, 3, "afaa"), (512, 768, 4, 4, "afaa"), (768, 1024, 5, 6, "afaa")),
+                ((256, 512, 2, 3, "afaa"), (512, 768, 4, 5, "afaa"), (768, 1024, 6, 7, "afav")),
+                ((512, 768, 2, 3, "aFav"), (768, 1024, 4, 5, "aFav")),
+                ((768, 1024, 2, 3, "aFav"),)),
+    "direct": True, "evac": ("aaavavavavavavvv",) * 4, "cast": (0, 0, 0, 0), "once": False,
+    "split": {}, "apart": (0, 0, 1, 2), "leave": True, "one": 7,
+    "whole": ((1,), (2, 3), (3,), ()), "early": ((1,), (), (), ()), "pair": ((), (), (), ()), "single": True,
+    "wide": (((1, 0),), (), (), ()), "again": 0, "cuts": 2, "chain": (0, 1, 3, 3), "load": "", "holds": True,
+    "fix": 5.0, "pfix": 0.0, "cyc": 0.83, "gat": 1.56, "hop": 220.0, "pe": 0.42, "rem": 700.0, "row": 20.0, "byte": (0.11, 0.08),
+    "issue": 300.0, "first": 1500.0, "fresh": 100.0, "t_in": 1600.0, "t_cs": 4500.0,
+    "t_ls": 5700.0, "t_g": 1000.0, "t_cast": 4000.0, "look": (100.0, 100.0, 100.0, 100.0), "prio": {}, "seed": 4, "tries": 100, "swaps": 700, "slack": 200.0,
 }
+
+
+def figures(gat, fv, fa, fp, pe, lp, hop, same, wake, issue, first, fresh, rem, row, byte, dq, t_in, t_cs, t_ls, t_y, t_v, cyc=0.83):
+    return {"cyc": cyc, "gat": gat, "fv": fv, "fa": fa, "fp": fp, "pe": pe, "lp": lp, "hop": hop, "same": same, "wake": wake, "issue": issue,
+            "first": first, "fresh": fresh, "rem": rem, "row": row, "byte": byte, "dq": dq,
+            "t": {"in": t_in, "csi": t_cs, "lsb": t_ls, "y": t_y, "vc": t_v, "dd": t_v + 500}}
+
+
+CFG["worlds"] = [
+    figures(1.56, 0, 10, 0, 0.42, 0, 230, 230, 250, 300, 1500, 100, (1000, 800), (20, 20), (0.07, 0.05), 50, 1600, 4500, 5700, 1500, 1500),
+    figures(1.56, 15, 25, 5, 0.42, 30, 200, 170, 300, 500, 1500, 100, (1400, 1200), (20, 20), (0.09, 0.05), 50, 1800, 5000, 6200, 1800, 1800),
+    figures(1.7, 10, 20, 5, 0.5, 30, 230, 230, 300, 400, 2000, 100, (1200, 1000), (30, 20), (0.09, 0.06), 80, 1800, 5500, 7000, 1800, 1800, 1.0),
+]
 
 F, I, H, B, U = "float32", "int32", "float16", "bfloat16", "uint16"
 SCRATCH = {k: ("sbuf", [128, n], t) for k, n, t in (
@@ -27,7 +41,7 @@ SCRATCH = {k: ("sbuf", [128, n], t) for k, n, t in (
     ("vf", 64, H), ("vc", 4096, H), ("vb", 1024, F), ("eni", 32, I), ("enf", 32, F), ("ent", 32, F),
     ("enm", 32, F), ("es", 384, F), ("land", 256, F), ("mine", 64, F), ("more", 256, F), ("o1", 384, U), ("o2", 384, U),
     ("xx", 1024, F), ("y1", 1024, F), ("y2", 1024, F), ("cg", 2048, F), ("lg", 1024, B), ("cmpb", 1024, B), ("yb", 1024, B),
-    ("tu", 2048, U), ("tin", 1536, U), ("tf", 1536, F), ("acc", 512, F))}
+    ("spare", 2048, B), ("tu", 2048, U), ("tw", 2048, F), ("tin", 1536, U), ("tf", 1536, F), ("acc", 1792, F))}
 for _h in range(1, NR):
     SCRATCH["vd%d" % _h] = ("dram", [128, 64], H)
 for _b in range(8):
@@ -90,8 +104,10 @@ def parts(a):
 
 def build(cores, topo, cfg):
     ops, hist, late = [], {}, []
-    CYC, GAT, HOP, CAST = cfg["cyc"], cfg["gat"], cfg["hop"], cfg["cast"]
-    LESS = 0.0 if CAST else MID
+    CYC, GAT, HOP = cfg["cyc"], cfg["gat"], cfg["hop"]
+
+    def less(q):
+        return 0.0 if cfg["cast"][q] else MID
     tag, ndma, nmsg = [None], [0] * NR, [0] * NR
 
     def add(q, eng, kind, args, busy, rd, wr, lat=0.0, sem=None, remote=None):
@@ -164,6 +180,9 @@ def build(cores, topo, cfg):
                     used.update(res[d])
         return res
 
+    def near(q, d):
+        return int(cores[d] in topo.cores_of(cores[q]))
+
     def send(q, items, leave=()):
         eng = split_engines(q, [it[0] for it in items], leave)
         sig, tr = {}, []
@@ -172,10 +191,11 @@ def build(cores, topo, cfg):
             sig[d] = ("m%d" % (nmsg[d] - 1), len(eng[d]))
             tr.append([cores[d], sum(1 << e for e in eng[d]), sig[d][0], src, dst])
         size = (items[0][1][2] - items[0][1][1]) * (4 if SCRATCH[items[0][1][0]][2] == F else 2)
-        lats = {d: cfg["rem"] + 128 / len(e) * (cfg["row"] + size * cfg["byte"]) for d, e in eng.items()}
+        lats = {d: cfg["rem"] + 128 / len(e) * (cfg["row"] + size * cfg["byte"][near(q, d)]) for d, e in eng.items()}
         i = add(q, "g", "send", (cores[q], tr), cfg["issue"], [(q, it[1]) for it in items], [(it[0], it[2]) for it in items],
                 lat=max(lats.values()), remote=sig)
         ops[i]["lats"], ops[i]["uses"] = lats, {e for v in eng.values() for e in v}
+        ops[i]["hold"] = [(e, lats[d] - cfg["rem"]) for d, v in eng.items() for e in v]
         return i
 
     (C_W, C_ODD, C_EVEN, C_LOW, C_16, C_T, C_K1, C_K2, C_TOP, C_S1, C_S2, C_WC, C_END) = range(13)
@@ -184,10 +204,10 @@ def build(cores, topo, cfg):
     CSI, CSF, LS = ap("csi", 0, 2064), ap("csf", 0, 2064), ap("lsb", 0, 2064)
 
     def floats(q):
-        return any(s[4][1] != "v" for s in cfg["streams"][q])
+        return any(s[4][1] in "af" for s in cfg["streams"][q])
 
     def start(q):
-        one, begin, z = ap("ones", 0, 128), len(ops), P * (NR - 1)
+        one, begin, z, CAST = ap("ones", 0, 128), len(ops), P * (NR - 1), cfg["cast"][q]
         t0 = cfg["t_in"]
         dma(q, "s", ap("bmc", 0, 512, 1, LO), ap("bm", 0, 4096, 1, EIGHT), t0, True)
         if not cfg["once"]:
@@ -196,6 +216,8 @@ def build(cores, topo, cfg):
         dma(q, "s", ap("eni", 0, 16), ap("en", 0, P, 1, EIGHT), t0 + 100, True)
         dma(q, "a", ap("eni", 16, 32), ap("en", 0, P, 1, EIGHT), t0 + 100, True)
         dma(q, "s", ap("csi", 8, 2056), ap("cs", 0, 2048), cfg["t_cs"], True)
+        if cfg["load"] == "d":
+            dma(q, "s", ap("spare", 0, 2048), ap("ls", 0, 2048), t0, True)
         loaded = dma(q, "s", ap("lsb", 8, 2056), ap("ls", 0, 2048), cfg["t_ls"], True)
         vec(q, "set", one, 1.0)
         fill(q, ap("zb", 0, 128), 0.0)
@@ -203,10 +225,10 @@ def build(cores, topo, cfg):
         def blocks(out, tmp, src):
             gp(q, "sel", ap(tmp, 0, 128), src, [[-16, 8], [0, 16]], A.is_ge, 0, 1)
             gp(q, "sel", ap(out, 0, 128), ap(tmp, 0, 128), [[16, 8], [0, 16]], A.is_ge, 15, -1)
-        gp(q, "iota", ap("ia", 0, 128), [[-8, 8], [0, 16]], 64, 1)
         gp(q, "iota", ap("i16", 0, 16), [[-1, 16]], 16, 1)
-        gp(q, "sel", ap("g8", 0, 128, 1, EIGHT), ap("ones", 0, 128, 1, EIGHT), [[-1, 8], [0, 16]], A.is_equal, 0, 1)
+        gp(q, "iota", ap("ia", 0, 128), [[-8, 8], [0, 16]], 64, 1)
         gp(q, "iotaf", ap("cc", 0, 256), [[-1, 256]], 0, 0)
+        gp(q, "sel", ap("g8", 0, 128, 1, EIGHT), ap("ones", 0, 128, 1, EIGHT), [[-1, 8], [0, 16]], A.is_equal, 0, 1)
         gp(q, "iotaf", ap("rr", 0, 128), [[0, 8], [1, 16]], -15, 0)
         gp(q, "sel", ap("idn", 0, 128), one, [[-1, 128]], A.is_equal, 0, 1)
         if CAST:
@@ -245,7 +267,9 @@ def build(cores, topo, cfg):
         act(q, col(C_S2), FIN, -CAP, -CAP / BIG)
         act(q, col(C_WC), FIN, -CAP, -16 * CAP / BIG)
         if q:
-            act(q, col(C_END), FIN, 5 * LESS, 4 * q * 2 * MID / BIG)
+            raw = sum(less(s) * (1 + part * (q in cfg["pair"][s])) for s in range(q) for part in (0, 1) if (q, part) in cfg["wide"][s]
+                      and (q not in cfg["whole"][s] if part else q in cfg["early"][s]))
+            act(q, col(C_END), FIN, 5 * less(q) + raw, 4 * q * 2 * MID / BIG)
         vec(q, "cp", ap("g8h", 0, 128, 1, EIGHT), ap("g8", 0, 128, 1, EIGHT))
         act(q, ap("r2", 0, 128), ap("rr", 0, 128), col(C_S2), col(C_S1))
         call(q, "a", "sign", (ap("r3", 0, 128), ap("rr", 0, 128)), 180)
@@ -278,16 +302,20 @@ def build(cores, topo, cfg):
         vec(q, "tt", last("dd", P * q, P * q + P), ap("enm", 0, 16), ap("enm", 16, 32), A.add)
         act(q, ap("pb7", 0, 512, 2), ap("cc", 0, 256), 0.0, col(C_LOW))
         act(q, ap("pb7", 1, 512, 2), ap("cc", 0, 256), col(C_16), col(C_LOW))
-        vec(q, "ts1", ap("bmt", 0, 512, 1, LO), ap("bmc", 0, 512, 1, LO), 5, A.logical_shift_right)
-        vec(q, "ts1", ap("bmt", 0, 512, 1, HI), ap("bmc", 0, 512, 1, LO if cfg["once"] else HI), 31, A.bitwise_and)
-        vec(q, "tt", ap("hl", 0, 512), ap("bmt", 0, 512), ap("pb7", 0, 512), A.add)
-        for o in range(8):
-            b, lo, c = ap("pb%d" % (2 + o % 5), 0, 512), 8 + 512 * o, -8192.0 * o - 65536.0 * q
-            mm(q, b, ap("sm", 128 * o, 128 * o + 128), ap("hl", 0, 512), True, True)
-            if cfg["evac"][q][o] == "a":
-                act(q, ap("yt", lo, lo + 512), b, c)
-            else:
-                built = vec(q, "ts1", ap("yt", lo, lo + 512), b, c, A.add)
+        m, k = 512 // cfg["cuts"], 0
+        for x in range(0, 512, m):
+            vec(q, "ts1", ap("bmt", x, x + m, 1, LO), ap("bmc", x, x + m, 1, LO), 5, A.logical_shift_right)
+            vec(q, "ts1", ap("bmt", x, x + m, 1, HI), ap("bmc", x, x + m, 1, LO if cfg["once"] else HI), 31, A.bitwise_and)
+            vec(q, "tt", ap("hl", x, x + m), ap("bmt", x, x + m), ap("pb7", x, x + m), A.add)
+        for x in range(0, 512, m):
+            for o in range(8):
+                b, lo, c = ap("pb%d" % (k % 7 if m < 512 else 2 + o % 5), 0, m), 8 + 512 * o + x, -8192.0 * o - 65536.0 * q
+                mm(q, b, ap("sm", 128 * o, 128 * o + 128), ap("hl", x, x + m), True, True)
+                if cfg["evac"][q][k] == "a":
+                    act(q, ap("yt", lo, lo + m), b, c)
+                else:
+                    built = vec(q, "ts1", ap("yt", lo, lo + m), b, c, A.add)
+                k += 1
         for i in range(begin, built if q else 0):
             if ops[i]["e"] == "v" and ops[i]["name"] == "csi":
                 late.append((i, built))
@@ -307,7 +335,7 @@ def build(cores, topo, cfg):
         vec(0, "ts2", at, ap("yt", 8, 9), 1.0 / 32, 8 + 16.5 / 32, A.mult, A.add)
         gather(0, "a", ap("zi", 0, 16), CSF, at)
         act(0, ap("csf", 0, 8), ap("zi", 0, 8))
-        vec(0, "ts1", ap("csi", 0, 8), ap("zi", 0, 8), LESS, A.add)
+        vec(0, "ts1", ap("csi", 0, 8), ap("zi", 0, 8), less(0), A.add)
         gather(0, "a", ap("zl", 0, 16), LS, at)
         act(0, ap("lsb", 0, 8), ap("zl", 0, 8))
 
@@ -333,14 +361,20 @@ def build(cores, topo, cfg):
         items = []
         for h, a, b in cut:
             x = P * (2 * q + part - h)
-            items.append((h, ap("tu", 1024 * part + a, 1024 * part + b), ap("tin", x + a, x + b)))
+            src, dst = ("tw", "tf") if (h, part) in cfg["wide"][q] else ("tu", "tin")
+            items.append((h, ap(src, 1024 * part + a, 1024 * part + b), ap(dst, x + a, x + b)))
             back[h].append((part, q, a - P * h, b - P * h))
-        send(q, items, far if cfg["leave"] else ())
+        send(q, items, far if cfg["leave"] and part else ())
 
     def state(q, t, lo, hi):
         return wrapped("es", t, lo, hi) if q else last("dd", lo, hi)
 
-    def task(q, t, lo, hi, ba, bb, on):
+    def report(q, src, dst, to):
+        for run in (to[:cfg["apart"][q]], to[cfg["apart"][q]:]):
+            if run:
+                send(q, [(d, src, dst) for d in run])
+
+    def task(q, t, lo, hi, ba, bb, on, lo2, hi2):
         n, own = hi - lo, lo // P == q
         if t == 1 and not own:
             vec(q, "ts1", state(q, 1, lo, hi), wrapped("land", 0, lo, hi), col(C_TOP), A.min)
@@ -352,20 +386,29 @@ def build(cores, topo, cfg):
             (vec(q, "cp", last("dd", lo, hi), E) if on[3] == "v" else act(q, last("dd", lo, hi), E))
         gather(q, on[0], XX, ap("yt", 0, 4112), O1)
         vec(q, "scan", Y1, XX, DD)
+        if q == 0 and lo >= 2 * P and t < 4 and cfg["load"] in ("v", "a"):
+            (vec(q, "cp", ap("vb", lo, hi), XX) if cfg["load"] == "v" else act(q, ap("vb", lo, hi), XX))
         vec(q, "ts2", O2, last("y1", lo, hi), 1.0 / 32, col(C_K2), A.mult, A.add)
-        zc = 1024 * (t % 2)
+        cg, zc, CAST, LESS = "cg", 1024 * (t % 2), cfg["cast"][q], less(q)
+        if t == 1 and lo // P in cfg["early"][q] and (lo // P, 0) in cfg["wide"][q]:
+            cg, zc = "tw", 0
         fused = on[1] in "fF" and t < 4
         cs_on = "v" if t == 0 or on[1] in "vF" else "a"
 
         def sections(a, b):
-            gather(q, cs_on, ap("cg", zc + a, zc + b), CSF if cs_on == "a" else CSI, wrapped("o2", t, a, b), -LESS)
+            gather(q, cs_on, ap(cg, zc + a, zc + b), CSF if cs_on == "a" else CSI, wrapped("o2", t, a, b), -LESS)
         if t == 4 and not own:
             for h, a, b in chunks(lo, hi):
                 if h in cfg["whole"][q]:
                     sections(a, b)
                     tally(q, a, b, ap("cg", zc + a, zc + b))
                 else:
-                    gather(q, "v", ap("tu", 1024 + a, 1024 + b), CSI, wrapped("o2", t, a, b))
+                    if h in cfg["pair"][q]:
+                        vec(q, "tt", ap("tw", 1024 + a, 1024 + b), ind(CSF, wrapped("o2", t, a, b)), ap("cg", 1024 + a, 1024 + b), A.add)
+                    elif (h, 1) in cfg["wide"][q]:
+                        gather(q, "a", ap("tw", 1024 + a, 1024 + b), CSF, wrapped("o2", t, a, b))
+                    else:
+                        gather(q, "v", ap("tu", 1024 + a, 1024 + b), CSI, wrapped("o2", t, a, b))
                     give_back(q, 1, a, b)
             return
         if not fused:
@@ -374,13 +417,15 @@ def build(cores, topo, cfg):
             LG, CM, YB = ap("lg", lo, hi), ap("cmpb", lo, hi), ap("yb", lo, hi)
             PA, PX = ap("pb%d" % ba, 0, n), ap("pb%d" % bb, P * (ba == bb), P * (ba == bb) + n)
             mm(q, PA, ap("g8h", 0, 128, 1, EIGHT), ap("vc", 4 * lo + t, 4 * hi, 4, EIGHT), True, fused or not CAST)
+            for _ in range(cfg["again"] * (q == 0)):
+                mm(q, PA, ap("g8h", 0, 128, 1, EIGHT), ap("vc", 4 * lo + t, 4 * hi, 4, EIGHT), True, True)
             if fused:
                 act(q, ap("vb", lo, hi), PA, MID)
                 vec(q, "tt", CM, ind(CSI, O2), ap("vb", lo, hi), A.is_gt)
             else:
                 if CAST:
                     mm(q, PA, ap("mid", 0, 128, 1, (0, 1)), ap("onb", 0, n, 1, (0, 1)), False, True)
-                vec(q, "tt", CM, ap("cg", zc + lo, zc + hi), PA, A.is_gt)
+                vec(q, "tt", CM, ap(cg, zc + lo, zc + hi), PA, A.is_gt)
             gather(q, on[2], LG, LS, O2)
             mm(q, PX, ap("wk", 0, 128), CM, True, False)
             pick = mm(q, PX, ap("idb", 0, 128), LG, False, True)
@@ -397,10 +442,8 @@ def build(cores, topo, cfg):
             if own:
                 if q > 0:
                     act(q, ES, NEW)
-                    if t or cfg["apart"]:
-                        send(q, [(q - 1, ES, LAND)])
-                    if t == 0 and lower[cfg["apart"]:]:
-                        send(q, [(d, ES, LAND) for d in lower[cfg["apart"]:]])
+                    if lo2 < hi2:
+                        report(q, state(q, t + 1, lo2, hi2), wrapped("land", t, lo2, hi2), lower if t == 0 else lower[:1])
             elif direct and q < NR - 2:
                 mine = wrapped("mine", 0, lo, hi)
                 if q > 0:
@@ -413,66 +456,78 @@ def build(cores, topo, cfg):
             else:
                 vec(q, "tt", ES, LAND, NEW, A.min)
                 if q > 0:
-                    send(q, [(d, ES, LAND) for d in (lower if direct else lower[:1])])
+                    report(q, ES, LAND, lower if direct else lower[:1])
             if fused:
                 sections(lo, hi)
         for h, a, b in chunks(lo, hi):
             if t == 1 and h in cfg["early"][q]:
-                vec(q, "ts1", ap("tu", a, b), ap("cg", zc + a, zc + b), LESS, A.add)
+                if cg == "cg":
+                    vec(q, "ts1", ap("tu", a, b), ap(cg, zc + a, zc + b), LESS, A.add)
                 give_back(q, 0, a, b)
                 continue
-            tally(q, a, b, ap("cg", zc + a, zc + b))
+            if t == 3 and h in cfg["pair"][q]:
+                continue
+            tally(q, a, b, ap(cg, zc + a, zc + b))
             if t < 4:
                 ops[-1]["deps"].add(pick)
 
-    def sums(q, whole):
-        hs = [h for h in range(q + 1, NR) if (h in cfg["whole"][q]) == whole]
-        for run in ([h for h in hs if h >= 2], [h for h in hs if h < 2]):
+    def sums(q, upto):
+        hs = [h for h in range(q + 1, NR) if upto == (4 if h in cfg["whole"][q] else 2 if h in cfg["pair"][q] else 3)]
+        for run in [[h] for h in hs[::-1]] if cfg["single"] else ([h for h in hs if h >= 2], [h for h in hs if h < 2]):
             if run:
                 a, e = P * run[0], P * run[-1] + P
                 b, x = sum_at(q, a, a)[:2]
                 part = int(run[0] in cfg["early"][q])
-                vec(q, "ts1", ap("tu", 1024 * part + a, 1024 * part + e), ap(b, x, x + e - a), (4 - part if whole else 3) * LESS, A.add)
+                plus = (upto - part) * less(q)
+                if (run[0], part) in cfg["wide"][q]:
+                    act(q, ap("tw", 1024 * part + a, 1024 * part + e), ap(b, x, x + e - a), plus)
+                else:
+                    vec(q, "ts1", ap("tu", 1024 * part + a, 1024 * part + e), ap(b, x, x + e - a), plus, A.add)
                 give_back(q, part, a, e)
 
     def finish(q):
         OWN, ACC = ap("pb0", 0, P), ap("acc", 0, P)
-        for part, s, a, b in sorted(back[q]):
-            if s > 0:
-                x = P * (2 * s + part)
-                vec(q, "cp", ap("tf", x + a, x + b), ap("tin", x + a, x + b))
-                tally(q, P * q + a, P * q + b, ap("tf", x + a, x + b))
-        if q:
-            vec(q, "ts1", ap("tf", 0, P), ap("tin", 0, P), col(C_END), A.add)
-            vec(q, "tt", ACC, OWN, ap("tf", 0, P), A.add)
-        else:
-            act(q, ACC, OWN, 5 * LESS)
-        ends = [(a, b) for part, s, a, b in back[q] if s == 0 and part == 1]
-        for a, b in ends:
-            vec(q, "cp", ap("pb7", a, b), ap("tin", P + a, P + b))
-            vec(q, "tt", ap("acc", P + a, P + b), ap("acc", a, b), ap("pb7", a, b), A.add)
-            dma(q, "s", ap("y", a, b), ap("acc", P + a, P + b), 1500 + 2 * (b - a))
-        if not ends:
+
+        def when(part, s):
+            return -9 if q in cfg["early"][s] and not part else 1.5 * (part or q in cfg["whole"][s]) - s
+        come = sorted({(when(part, s), part, s) for part, s, _, _ in back[q]})
+        cut = max(0, len(come) - cfg["chain"][q])
+        for _, part, s in come[:cut]:
+            x = P * (2 * s + part)
+            if (q, part) not in cfg["wide"][s]:
+                vec(q, "cp", ap("tf", x, x + P), ap("tin", x, x + P))
+            tally(q, P * q, P * q + P, ap("tf", x, x + P))
+        act(q, ACC, OWN, col(C_END) if q else 5 * less(q))
+        for k, (_, part, s) in enumerate(come[cut:]):
+            x, pb = P * (2 * s + part), "pb%d" % (2 + k)
+            for a, b in sorted(c[2:] for c in back[q] if c[:2] == (part, s)):
+                vec(q, "cp", ap(pb, a, b), ap("tin", x + a, x + b))
+                vec(q, "tt", ap("acc", P * k + P + a, P * k + P + b), ap("acc", P * k + a, P * k + b), ap(pb, a, b), A.add)
+                if k == len(come) - cut - 1:
+                    dma(q, "s", ap("y", a, b), ap("acc", P * k + P + a, P * k + P + b), 1500 + 2 * (b - a))
+        if not come:
             dma(q, "s", ap("y", 0, P), ACC, 2000)
 
     for q in range(NR):
         start(q)
     for rnd in range(6):
         for q in range(NR - 1, -1, -1):
-            if rnd == 5:
-                sums(q, False)
+            if rnd >= 4:
+                sums(q, rnd - 2)
             for k, s in reversed(list(enumerate(cfg["streams"][q]))):
                 t = rnd if s[0] // P == q else rnd - 1
                 if t <= 4 and (t > 0 or t == rnd):
-                    tag[0] = "%d%d%d" % (q, rnd, k)
-                    task(q, t, *s)
+                    cut = cfg["split"].get((q, t)) if s[0] // P == q else None
+                    for x, piece in enumerate(cut or [s]):
+                        tag[0] = "%d%d%d" % (q, rnd, k) + "abcd"[x] * bool(cut)
+                        task(q, t, *piece, *((s[0], s[1]) if cut and x == len(cut) - 1 else (0, 0) if cut else piece[:2]))
                     tag[0] = None
             if rnd == 0:
                 visitors_v(q)
                 if q == 0:
                     zero_bin()
             if rnd == 5:
-                sums(q, True)
+                sums(q, 4)
     for q in range(NR):
         finish(q)
 
@@ -532,10 +587,148 @@ def build(cores, topo, cfg):
         if res[0] <= now[0] + cfg["slack"] * (1 - step / cfg["tries"]):
             prio, now = trial, res
             best = min(best, res, key=lambda x: x[0])
-    end, at = best
+    order = sorted(range(n), key=lambda i: (best[1][i], i))
+
+    above, before = [0] * n, [[] for _ in range(n)]
+    place = {i: k for k, i in enumerate(order)}
+    for i in range(n):
+        for u, d in gap[i]:
+            before[u].append((i, d))
+    for i in order:
+        keep = []
+        for j, d in sorted(before[i], key=lambda x: -place[x[0]]):
+            if not above[i] >> j & 1 or ops[j]["lat"] > HOP:
+                keep.append((j, d))
+                above[i] |= above[j] | 1 << j
+        before[i] = keep
+    busy, lat, uses = [o["busy"] for o in ops], [o["lat"] for o in ops], [o.get("uses") for o in ops]
+
+    def replay(order):
+        fin, why, prev, free, used, end, top = [0.0] * n, [0] * n, [-1] * (5 * NR), [0.0] * (5 * NR), [set() for _ in range(5 * NR)], 0.0, 0
+        rows = {}
+        for i in order:
+            k = queue[i]
+            t, w = free[k], -2 - prev[k]
+            for j, d in before[i]:
+                if fin[j] + d > t:
+                    t, w = fin[j] + d, j
+            t += busy[i]
+            if uses[i]:
+                t += (0.0 if used[k] else cfg["first"]) + cfg["fresh"] * len(uses[i] - used[k])
+                used[k] |= uses[i]
+            free[k] = t
+            if uses[i] and cfg["holds"]:
+                t = max([t] + [rows.get((k, e), 0.0) for e in uses[i]])
+                for e, d in ops[i]["hold"]:
+                    rows[(k, e)] = t + d
+            fin[i] = t
+            prev[k], why[i] = i, w
+            if t + lat[i] > end:
+                end, top = t + lat[i], i
+        return end, fin, why, top
+
+    def price(w):
+        bs, ls, tr = [], [], []
+        for o in ops:
+            picks = any(a[0] == "@" for a in o["args"] if isinstance(a, tuple))
+            moves = []
+            if o["rem"]:
+                b, l = w["issue"], 0.0
+                for core, mask, _, a, _ in o["args"][1]:
+                    d = cores.index(core)
+                    x, es = near(o["q"], d), [16 * o["q"] + e for e in range(16) if mask >> e & 1]
+                    size = (a[2] - a[1]) * (4 if SCRATCH[a[0]][2] == F else 2)
+                    moves.append((d, es, w["rem"][x], 128 / len(es) * (w["row"][x] + size * w["byte"][x])))
+            elif o["sem"]:
+                b, l = (w["dq"], w["t"].get(o["name"], w["t"]["in"])) if o["e"] != "g" else (o["busy"], o["lat"])
+            elif o["e"] in "va":
+                b, l = w["f" + o["e"]] + (o["busy"] - cfg["fix"] - 15 * (o["e"] == "a")) / CYC * w["cyc"] * (w["gat"] / GAT if picks else 1), 0.0
+            elif o["e"] == "p":
+                b, l = w["fp"] + (o["busy"] - cfg["pfix"]) / cfg["pe"] * w["pe"], w["lp"]
+            else:
+                b, l = o["busy"] * w["cyc"] / CYC, 0.0
+            bs.append(b)
+            ls.append(l)
+            tr.append(moves)
+        edges = [[(n + NR * j + o["q"], j, w["wake"]) if ops[j]["rem"] else
+                  (j, j, ls[j] + w["hop"] if queue[j] != queue[i] or ops[j]["sem"] else 0.0 if o["e"] in "pg" else w["same"])
+                  for j, _ in before[i]] for i, o in enumerate(ops)]
+        return bs, ls, tr, edges, w["first"], w["fresh"]
+
+    def walk(order, bs, ls, tr, edges, first, fresh):
+        fin, why, prev, free, rows = [0.0] * (n * (NR + 1)), [0] * n, [-1] * (5 * NR), [0.0] * (5 * NR), [-1.0] * (16 * NR)
+        end, top, called = 0.0, 0, [False] * (5 * NR)
+        for i in order:
+            k = queue[i]
+            t, w = free[k], -2 - prev[k]
+            for x, j, d in edges[i]:
+                if fin[x] + d > t:
+                    t, w = fin[x] + d, j
+            t += bs[i]
+            if tr[i]:
+                t += (0.0 if called[k] else first) + fresh * sum(rows[e] < 0 for m in tr[i] for e in m[1])
+                called[k] = True
+                for d, es, start, span in tr[i]:
+                    s = max([t + start] + [rows[e] for e in es]) + span
+                    for e in es:
+                        rows[e] = s
+                    fin[n + NR * i + d] = s
+            fin[i] = free[k] = t
+            prev[k], why[i] = i, w
+            if t + ls[i] > end:
+                end, top = t + ls[i], i
+        return end, fin, why, top
+
+    if cfg["worlds"]:
+        prices, turn = [price(w) for w in cfg["worlds"]], [0]
+        busy = prices[0][0]
+
+        def replay(order):
+            runs = [walk(order, *p) for p in prices]
+            turn[0] += 1
+            return (sum(r[0] for r in runs) / len(runs), runs[0][1]) + runs[turn[0] % len(runs)][2:]
+
+    def swap(order, u, v):
+        a, b = order.index(u), order.index(v)
+        front, behind, moved, held = [], [], 0, set()
+        for x in order[a:b]:
+            if x == u or above[x] & moved or queue[x] in held:
+                behind.append(x)
+                moved |= 1 << x
+                held.add(queue[x])
+            else:
+                front.append(x)
+        return None if above[v] & moved else order[:a] + front + [v] + behind + order[b + 1:]
+
+    now = best = (replay(order), order)
+    barred = {}
+    for step in range(cfg["swaps"]):
+        pairs, i = [], now[0][3]
+        while now[0][2][i] != -1:
+            w = now[0][2][i]
+            if w < -1:
+                w = -2 - w
+                if not above[i] >> w & 1 and "boost" not in ops[w]:
+                    seed = (seed * 1103515245 + 12345) % 2147483648
+                    pairs.append((seed >> 8, w, i))
+            i = w
+        found = None
+        for _, u, v in sorted(pairs)[:12]:
+            new = swap(now[1], u, v)
+            res = new and replay(new)
+            if res and (barred.get((v, u), -1) < step or res[0] < best[0][0]) and (not found or res[0] < found[0][0]):
+                found = (res, new, u, v)
+                if res[0] < now[0][0] - 1:
+                    break
+        if found:
+            barred[found[2:]] = step + 8 + seed % 8
+            now = found[:2]
+            best = min(best, now, key=lambda x: x[0][0])
+        else:
+            now, barred = best, {}
+    (end, fin, _, _), order = best
     for i, o in enumerate(ops):
-        o["t"] = at[i]
-    order = sorted(range(n), key=lambda i: (at[i], i))
+        o["t"] = fin[i] - busy[i]
     count, closing = {}, {}
     for i in order:
         o = ops[i]
@@ -573,29 +766,26 @@ def rank_program(g, core, T, topo):
         PLAN["p"] = build(list(T.cores), topo, CFG)
     ops, order, _ = PLAN["p"]
     queue = {"g": g, "v": g.vector, "a": g.scalar, "p": g.tensor, "s": g.sync}
-    seen, total = {}, {}
+    seen, total, knew, waited, place = {}, {}, {}, set(), {i: k for k, i in enumerate(order)}
     for i in order:
         o = ops[i]
         if o["rem"] and q in o["rem"]:
             total[o["rem"][q][0]] = o["rem"][q][1]
         if o["q"] != q:
             continue
-        need = {}
-        for j in o["deps"]:
+        know = seen.setdefault(o["e"], {})
+        for j in sorted(o["deps"], key=lambda j: -place[j]):
             d = ops[j]
-            if d["rem"]:
-                s, v = d["rem"][q]
-            elif d["e"] == "p" and o["e"] == "p":
+            if d["e"] == o["e"] and (d["e"] == "p" or d["e"] == "g" and not d["rem"] and (o["rem"] or d["args"][0] not in o["args"])):
                 continue
-            elif d["e"] == "g" and o["e"] == "g" and (o["rem"] or d["args"][0] not in o["args"]):
-                continue
-            else:
-                s, v = d["sig"]
-            need[s] = max(need.get(s, 0), v)
-        for s, v in need.items():
-            if seen.get((o["e"], s), 0) < v:
-                seen[(o["e"], s)] = v
+            s, v = d["rem"][q] if d["rem"] else d["sig"]
+            if know.get(s, 0) < v:
                 queue[o["e"]].wait_ge(T.sem[s], v)
+                waited.add((o["e"], s, v))
+                know[s] = v
+                for s2, v2 in knew.get(j, {}).items():
+                    know[s2] = max(know.get(s2, 0), v2)
+        knew[i] = dict(know)
         r = emit(g, T, o, topo)
         if o["rem"]:
             total["sent"] = total.get("sent", 0) + sum(v for _, v in o["rem"].values())
@@ -603,5 +793,5 @@ def rank_program(g, core, T, topo):
             r.then_inc(T.sem[o["sig"][0]], 16 if o["sem"] else 1)
             total[o["sig"][0]] = o["sig"][1]
     for s, v in total.items():
-        if seen.get(("g", s), 0) < v:
+        if ("g", s, v) not in waited:
             g.wait_ge(T.sem[s], v)

from concourse.bass import DstId, RemoteDMATransfer
from concourse.mybir import AluOpType as A, ActivationFunctionType as AF

NR, P, W = 4, 256, 16
BIG, HUGE, OUT, CAP, MID = float(1 << 20), float(1 << 22), float(1 << 19), float(1 << 18), 2048.0
CFG = {
    "streams": (((0, 256, 2, 2, "afaa"), (256, 512, 3, 3, "afaa"), (512, 768, 4, 4, "afaa"), (768, 1024, 5, 6, "afaa")),
                ((256, 512, 2, 3, "afaa"), (512, 768, 4, 5, "afaa"), (768, 1024, 6, 7, "afav")),
                ((512, 768, 2, 3, "aFav"), (768, 1024, 4, 5, "aFav")),
                ((768, 1024, 2, 3, "aFav"),)),
    "direct": True, "evac": ("aaavavavavavavvv",) * 4, "cast": (0, 0, 0, 0), "once": False,
    "split": {}, "apart": (0, 0, 1, 2), "leave": True, "one": 7,
    "whole": ((1,), (2, 3), (3,), ()), "early": ((1,), (), (), ()), "pair": ((), (), (), ()), "single": True,
    "wide": (((1, 0),), (), (), ()), "again": 0, "cuts": 2, "chain": (0, 1, 3, 3), "load": "", "holds": True,
    "fix": 5.0, "pfix": 0.0, "cyc": 0.83, "gat": 1.56, "hop": 220.0, "pe": 0.42, "rem": 700.0, "row": 20.0, "byte": (0.11, 0.08),
    "issue": 300.0, "first": 1500.0, "fresh": 100.0, "t_in": 1600.0, "t_cs": 4500.0,
    "t_ls": 5700.0, "t_g": 1000.0, "t_cast": 4000.0, "look": (100.0, 100.0, 100.0, 100.0), "prio": {}, "seed": 4, "tries": 100, "swaps": 700, "slack": 200.0,
}


def figures(gat, fv, fa, fp, pe, lp, hop, same, wake, issue, first, fresh, rem, row, byte, dq, t_in, t_cs, t_ls, t_y, t_v, cyc=0.83):
    return {"cyc": cyc, "gat": gat, "fv": fv, "fa": fa, "fp": fp, "pe": pe, "lp": lp, "hop": hop, "same": same, "wake": wake, "issue": issue,
            "first": first, "fresh": fresh, "rem": rem, "row": row, "byte": byte, "dq": dq,
            "t": {"in": t_in, "csi": t_cs, "lsb": t_ls, "y": t_y, "vc": t_v, "dd": t_v + 500}}


CFG["worlds"] = [
    figures(1.56, 0, 10, 0, 0.42, 0, 230, 230, 250, 300, 1500, 100, (1000, 800), (20, 20), (0.07, 0.05), 50, 1600, 4500, 5700, 1500, 1500),
    figures(1.56, 15, 25, 5, 0.42, 30, 200, 170, 300, 500, 1500, 100, (1400, 1200), (20, 20), (0.09, 0.05), 50, 1800, 5000, 6200, 1800, 1800),
    figures(1.7, 10, 20, 5, 0.5, 30, 230, 230, 300, 400, 2000, 100, (1200, 1000), (30, 20), (0.09, 0.06), 80, 1800, 5500, 7000, 1800, 1800, 1.0),
]

F, I, H, B, U = "float32", "int32", "float16", "bfloat16", "uint16"
SCRATCH = {k: ("sbuf", [128, n], t) for k, n, t in (
    ("bmc", 512, I), ("bmt", 512, I), ("cc", 256, F), ("hl", 512, H), ("yt", 4112, F), ("csi", 2064, I), ("csf", 2064, F),
    ("lsb", 2064, B), ("ia", 128, I), ("ib", 128, I), ("ibh", 128, H), ("sm", 1024, H), ("ones", 128, F), ("rr", 128, F),
    ("r1", 128, B), ("r2", 128, B), ("r3", 128, F), ("r4", 128, B), ("t1", 128, B), ("t2", 128, B), ("t4", 128, B),
    ("wk", 128, B), ("wy", 128, B), ("wc", 128, B), ("idb", 128, B), ("zb", 128, B), ("idn", 128, F), ("g8", 128, F),
    ("g8h", 128, H), ("onb", 512, B), ("mid", 128, B), ("i16", 16, I), ("j16", 16, I), ("j1", 8, I), ("col", 128, F),
    ("da", 16, F), ("db", 16, F), ("dd", 1024, F), ("oz", 8, U), ("zi", 16, F), ("zl", 16, B), ("sdi", 16, I), ("vi", 64, I),
    ("vf", 64, H), ("vc", 4096, H), ("vb", 1024, F), ("eni", 32, I), ("enf", 32, F), ("ent", 32, F),
    ("enm", 32, F), ("es", 384, F), ("land", 256, F), ("mine", 64, F), ("more", 256, F), ("o1", 384, U), ("o2", 384, U),
    ("xx", 1024, F), ("y1", 1024, F), ("y2", 1024, F), ("cg", 2048, F), ("lg", 1024, B), ("cmpb", 1024, B), ("yb", 1024, B),
    ("spare", 2048, B), ("tu", 2048, U), ("tw", 2048, F), ("tin", 1536, U), ("tf", 1536, F), ("acc", 1792, F))}
for _h in range(1, NR):
    SCRATCH["vd%d" % _h] = ("dram", [128, 64], H)
for _b in range(8):
    SCRATCH["pb%d" % _b] = ("psum", [128, 512], F)

SEMAPHORES = ["nv", "na", "nt", "ng", "sent"] + ["d%d" % i for i in range(32)] + ["m%d" % i for i in range(60)]
COUNT = {"v": "nv", "a": "na", "p": "nt", "g": "ng"}
CALLS = {
    "set": lambda g, o, c: g.vector.memset(o, c),
    "cp": lambda g, o, i: g.vector.tensor_copy(o, i),
    "tt": lambda g, o, a, b, op: g.vector.tensor_tensor(o, a, b, op),
    "ts1": lambda g, o, a, s, op: g.vector.tensor_scalar(o, a, s, None, op),
    "ts2": lambda g, o, a, s1, s2, op0, op1: g.vector.tensor_scalar(o, a, s1, s2, op0, op1),
    "scan": lambda g, o, a, b: g.vector.tensor_tensor_scan(o, a, b, HUGE, A.min, A.add),
    "tr": lambda g, o, i: g.vector.transpose(o, i),
    "acp": lambda g, o, i, s: g.scalar.activation(o, i, AF.Copy, scale=s),
    "aid": lambda g, o, i, b, s: g.scalar.activation(o, i, AF.Identity, bias=b, scale=s),
    "sign": lambda g, o, i: g.scalar.activation(o, i, AF.Sign),
    "mm": lambda g, o, l, r, start, stop: g.tensor.matmul(o, l, r, start, stop),
    "iota": lambda g, o, pat, base, cm: g.iota(o, pat, base, cm),
    "iotaf": lambda g, o, pat, base, cm: g.iota(o, pat, base, cm, allow_small_or_imprecise_dtypes=True),
    "sel": lambda g, o, i, pat, op, base, cm: g.affine_select(o, i, pat, op, 0.0, base, cm),
    "g": lambda g, o, i: g.dma_start(o, i),
    "s": lambda g, o, i: g.sync.dma_start(o, i),
    "a": lambda g, o, i: g.scalar.dma_start(o, i),
}


def ap(name, lo, hi, step=1, rows=(0, 128)):
    return (name, lo, hi, step, rows[0], rows[1])


def ind(win, off):
    return ("@", win, off)


def col(k, rows=(0, 128)):
    return ap("col", 4 * k, 4 * k + 1, 1, rows)


def last(name, lo, hi):
    return ap(name, lo + W - 1, hi, W)


def wrapped(name, k, lo, hi):
    return ap(name, 64 * k + lo // W, 64 * k + hi // W)


def real(T, a):
    if not isinstance(a, tuple):
        return a
    if a[0] == "@":
        return real(T, a[1]).indirect(real(T, a[2]))
    return T[a[0]][a[4]:a[5], a[1]:a[2]:a[3]] if a[3] > 1 else T[a[0]][a[4]:a[5], a[1]:a[2]]


def parts(a):
    return [] if not isinstance(a, tuple) else [a[1], a[2]] if a[0] == "@" else [a]


def build(cores, topo, cfg):
    ops, hist, late = [], {}, []
    CYC, GAT, HOP = cfg["cyc"], cfg["gat"], cfg["hop"]

    def less(q):
        return 0.0 if cfg["cast"][q] else MID
    tag, ndma, nmsg = [None], [0] * NR, [0] * NR

    def add(q, eng, kind, args, busy, rd, wr, lat=0.0, sem=None, remote=None):
        i, deps = len(ops), set()
        for acc, write in ((rd, False), (wr, True)):
            for r, (name, lo, hi, _, r0, r1) in acc:
                for (j, e2, l2, h2, a2, b2, w2) in hist.setdefault((r, name), []):
                    meet = lo < h2 and l2 < hi and r0 < b2 and a2 < r1 and (write or w2)
                    if j != i and (meet or (name.startswith("pb") and e2 != eng)):
                        deps.add(j)
                hist[(r, name)].append((i, eng, lo, hi, r0, r1, write))
        ops.append({"q": q, "e": eng, "kind": kind, "args": list(args), "busy": busy, "lat": lat, "deps": deps, "sem": sem,
                    "rem": remote, "name": wr[0][1][0], "tag": tag[0]})
        return i

    def call(q, eng, kind, args, busy, **kw):
        rd = [(q, x) for a in args[1:] for x in parts(a)]
        return add(q, eng, kind, args, busy, rd, [(q, args[0])], **kw)

    def width(a):
        return W * width(a[2]) * GAT if a[0] == "@" else (a[2] - a[1] + a[3] - 1) // a[3]

    def vec(q, kind, *args):
        n = width(args[0] if kind == "set" else args[1])
        if kind == "tt" and args[1][0] != "@" and not (args[1][0].startswith("pb") or args[2][0].startswith("pb")):
            n *= 2
        return call(q, "v", kind, args, cfg["fix"] + max(64, n) * CYC)

    def act(q, out, src, bias=None, scale=1.0):
        busy = cfg["fix"] + 15 + max(64, width(src)) * CYC
        return call(q, "a", "acp", (out, src, scale), busy) if bias is None else call(q, "a", "aid", (out, src, bias, scale), busy)

    def mm(q, out, lhs, rhs, start, stop):
        slow = 4 if SCRATCH[rhs[0]][2] == F else 1
        return call(q, "p", "mm", (out, lhs, rhs, start, stop), cfg["pfix"] + max(64, width(rhs)) * slow * cfg["pe"], lat=40.0)

    def gp(q, kind, *args):
        rd = [(q, x) for a in args[1:] for x in parts(a)]
        return add(q, "g", kind, args, 150 + 2 * width(args[0]) * CYC, rd, [(q, args[0]), (q, ap("order", 0, 1))])

    def fill(q, out, c):
        return act(q, out, ap("ones", 0, width(out), 1, out[4:6]), None, c)

    def gather(q, eng, out, win, off, plus=None):
        if eng == "a":
            return act(q, out, ind(win, off))
        return vec(q, "cp", out, ind(win, off)) if not plus else vec(q, "ts1", out, ind(win, off), plus, A.add)

    def dma(q, eng, out, src, lat, boost=False):
        ndma[q] += 1
        i = add(q, eng, eng, (out, src), 80, [(q, src)], [(q, out)], lat=lat, sem=("d%d" % (ndma[q] - 1), 16))
        if boost:
            ops[i]["boost"] = 1e6 - 1e4 * ndma[q]
        return i

    def split_engines(q, dsts, leave):
        can = {d: topo.engines(cores[q], cores[d]) for d in list(dsts) + list(leave)}
        least = min(len(v) for v in can.values())
        used, res = set(), {}
        for d in leave:
            used.update(can[d])
        for part in ([d for d in dsts if len(can[d]) == least], [d for d in dsts if len(can[d]) > least]):
            if part:
                free = [e for e in can[part[0]] if e not in used and all(e in can[d] for d in part)]
                n = 1
                while 2 * n * len(part) <= len(free):
                    n *= 2
                for x, d in enumerate(part):
                    res[d] = free[x * n:(x + 1) * n]
                    used.update(res[d])
        return res

    def near(q, d):
        return int(cores[d] in topo.cores_of(cores[q]))

    def send(q, items, leave=()):
        eng = split_engines(q, [it[0] for it in items], leave)
        sig, tr = {}, []
        for d, src, dst in items:
            nmsg[d] += 1
            sig[d] = ("m%d" % (nmsg[d] - 1), len(eng[d]))
            tr.append([cores[d], sum(1 << e for e in eng[d]), sig[d][0], src, dst])
        size = (items[0][1][2] - items[0][1][1]) * (4 if SCRATCH[items[0][1][0]][2] == F else 2)
        lats = {d: cfg["rem"] + 128 / len(e) * (cfg["row"] + size * cfg["byte"][near(q, d)]) for d, e in eng.items()}
        i = add(q, "g", "send", (cores[q], tr), cfg["issue"], [(q, it[1]) for it in items], [(it[0], it[2]) for it in items],
                lat=max(lats.values()), remote=sig)
        ops[i]["lats"], ops[i]["uses"] = lats, {e for v in eng.values() for e in v}
        ops[i]["hold"] = [(e, lats[d] - cfg["rem"]) for d, v in eng.items() for e in v]
        return i

    (C_W, C_ODD, C_EVEN, C_LOW, C_16, C_T, C_K1, C_K2, C_TOP, C_S1, C_S2, C_WC, C_END) = range(13)
    FIRST, FIN = ap("db", 15, 16), ap("da", 15, 16)
    LO, HI, EIGHT = (0, 64), (64, 128), (0, 8)
    CSI, CSF, LS = ap("csi", 0, 2064), ap("csf", 0, 2064), ap("lsb", 0, 2064)

    def floats(q):
        return any(s[4][1] in "af" for s in cfg["streams"][q])

    def start(q):
        one, begin, z, CAST = ap("ones", 0, 128), len(ops), P * (NR - 1), cfg["cast"][q]
        t0 = cfg["t_in"]
        dma(q, "s", ap("bmc", 0, 512, 1, LO), ap("bm", 0, 4096, 1, EIGHT), t0, True)
        if not cfg["once"]:
            dma(q, "a", ap("bmc", 0, 512, 1, HI), ap("bm", 0, 4096, 1, EIGHT), t0, True)
        dma(q, "a", ap("sdi", 0, 16), ap("sd", 0, P, 1, EIGHT), t0, True)
        dma(q, "s", ap("eni", 0, 16), ap("en", 0, P, 1, EIGHT), t0 + 100, True)
        dma(q, "a", ap("eni", 16, 32), ap("en", 0, P, 1, EIGHT), t0 + 100, True)
        dma(q, "s", ap("csi", 8, 2056), ap("cs", 0, 2048), cfg["t_cs"], True)
        if cfg["load"] == "d":
            dma(q, "s", ap("spare", 0, 2048), ap("ls", 0, 2048), t0, True)
        loaded = dma(q, "s", ap("lsb", 8, 2056), ap("ls", 0, 2048), cfg["t_ls"], True)
        vec(q, "set", one, 1.0)
        fill(q, ap("zb", 0, 128), 0.0)

        def blocks(out, tmp, src):
            gp(q, "sel", ap(tmp, 0, 128), src, [[-16, 8], [0, 16]], A.is_ge, 0, 1)
            gp(q, "sel", ap(out, 0, 128), ap(tmp, 0, 128), [[16, 8], [0, 16]], A.is_ge, 15, -1)
        gp(q, "iota", ap("i16", 0, 16), [[-1, 16]], 16, 1)
        gp(q, "iota", ap("ia", 0, 128), [[-8, 8], [0, 16]], 64, 1)
        gp(q, "iotaf", ap("cc", 0, 256), [[-1, 256]], 0, 0)
        gp(q, "sel", ap("g8", 0, 128, 1, EIGHT), ap("ones", 0, 128, 1, EIGHT), [[-1, 8], [0, 16]], A.is_equal, 0, 1)
        gp(q, "iotaf", ap("rr", 0, 128), [[0, 8], [1, 16]], -15, 0)
        gp(q, "sel", ap("idn", 0, 128), one, [[-1, 128]], A.is_equal, 0, 1)
        if CAST:
            vec(q, "set", ap("onb", 0, P, 1, (0, 1)), 1.0)
            fill(q, ap("mid", 0, 128, 1, (0, 1)), MID)
        fill(q, col(C_W, LO), 32.0)
        fill(q, col(C_W, HI), -1.0)
        fill(q, col(C_LOW, LO), 1.0)
        fill(q, col(C_LOW, HI), 0.0)
        act(q, col(C_16), col(C_LOW), 16.0, -16.0)
        vec(q, "ts1", ap("ib", 0, 128), ap("ia", 0, 128), 63, A.bitwise_and)
        vec(q, "cp", ap("ibh", 0, 128), ap("ib", 0, 128))
        for o in range(8):
            vec(q, "ts2", ap("sm", 128 * o, 128 * o + 128), ap("ibh", 0, 128), float(o), col(C_W), A.is_equal, A.mult)
            ops[-1]["busy"] = cfg["fix"] + 64 * CYC
        vec(q, "ts1", ap("j16", 0, 16), ap("i16", 0, 16), 15, A.bitwise_and)
        vec(q, "ts2", ap("j1", 0, 1), ap("i16", 0, 1), 4, 1, A.logical_shift_right, A.bitwise_and)
        vec(q, "cp", col(C_EVEN), ap("j1", 0, 1))
        vec(q, "ts2", ap("da", 0, 16), ap("j16", 0, 16), 0.0, -BIG, A.is_equal, A.mult)
        vec(q, "ts2", ap("db", 0, 16), ap("j16", 0, 16), 1.0, HUGE, A.is_equal, A.mult)
        vec(q, "tt", ap("dd", z, z + 16), ap("da", 0, 16), ap("db", 0, 16), A.add)
        for n in (16, 32, 64, 128):
            act(q, ap("dd", z + n, z + 2 * n), ap("dd", z, z + n))
        for h in range(q, NR - 1):
            if h == q:
                act(q, ap("dd", P * h, P * h + P), ap("dd", z, z + P))
            else:
                late.append((dma(q, "s", ap("dd", P * h, P * h + P), ap("dd", z, z + P), 2500), loaded))
        act(q, col(C_ODD), col(C_EVEN), 1.0, -1.0)
        act(q, col(C_K1), FIRST, 8 - 7.5 / 16 - 4096.0 * q, -1.0 / 16)
        act(q, col(C_T), FIN, 8 + 16.5 / 32 + BIG / 32, 1.0 / 32)
        act(q, col(C_K2), FIRST, col(C_T), -1.0 / 32)
        if q < NR - 1:
            act(q, col(C_TOP), FIRST, 65536.0 * (q + 1))
        act(q, col(C_S1), FIN, None, CAP / BIG)
        act(q, col(C_S2), FIN, -CAP, -CAP / BIG)
        act(q, col(C_WC), FIN, -CAP, -16 * CAP / BIG)
        if q:
            raw = sum(less(s) * (1 + part * (q in cfg["pair"][s])) for s in range(q) for part in (0, 1) if (q, part) in cfg["wide"][s]
                      and (q not in cfg["whole"][s] if part else q in cfg["early"][s]))
            act(q, col(C_END), FIN, 5 * less(q) + raw, 4 * q * 2 * MID / BIG)
        vec(q, "cp", ap("g8h", 0, 128, 1, EIGHT), ap("g8", 0, 128, 1, EIGHT))
        act(q, ap("r2", 0, 128), ap("rr", 0, 128), col(C_S2), col(C_S1))
        call(q, "a", "sign", (ap("r3", 0, 128), ap("rr", 0, 128)), 180)
        act(q, ap("r4", 0, 128), ap("r3", 0, 128), col(C_WC), FIN)
        fill(q, ap("r1", 0, 128), -1.0)
        blocks("wk", "t2", ap("r2", 0, 128))
        blocks("wc", "t4", ap("r4", 0, 128))
        blocks("wy", "t1", ap("r1", 0, 128))
        act(q, ap("idb", 0, 128), ap("idn", 0, 128))
        fill(q, ap("yt", 0, 8), -OUT)
        fill(q, ap("yt", 4104, 4112), -OUT if q else -16.0)
        for x in (0, 2056):
            vec(q, "ts2", ap("csi", x, x + 8), ap("ones", 0, 8), FIN, -2 * MID / BIG, A.mult, A.mult)
            fill(q, ap("lsb", x, x + 8), 0.0)
        if CAST and floats(q):
            dma(q, "g", CSF, CSI, cfg["t_cast"])
            ops[-1]["busy"] = cfg["t_g"]
        for t in range(4):
            i = vec(q, "ts2", ap("vi", t, 64, 4), ap("sdi", 0, 16), 4 * t, 4095, A.logical_shift_right, A.bitwise_and)
            ops[i]["deps"] = {j for j in ops[i]["deps"] if ops[j]["name"] != "vi"}
        vec(q, "ts1", ap("vf", 0, 64), ap("vi", 0, 64), -MID, A.add)
        dma(q, "s", ap("vc", 4 * P * q, 4 * P * (q + 1), 1, EIGHT), ap("vf", 0, 64), 2200)
        if q > 0:
            i = send(q, [(d, ap("vf", 0, 64), ap("vd%d" % q, 0, 64)) for d in range(q - 1, -1, -1)])
            ops[i]["deps"].add(max(j for j in range(begin, i) if ops[j]["kind"] == "sel"))
        vec(q, "cp", ap("enf", 0, 32), ap("eni", 0, 32))
        vec(q, "tr", ap("ent", 0, 32), ap("enf", 0, 32))
        act(q, ap("enm", 0, 16), ap("ent", 0, 16), FIRST, col(C_EVEN))
        act(q, ap("enm", 16, 32), ap("ent", 16, 32), 0.0, col(C_ODD))
        vec(q, "tt", last("dd", P * q, P * q + P), ap("enm", 0, 16), ap("enm", 16, 32), A.add)
        act(q, ap("pb7", 0, 512, 2), ap("cc", 0, 256), 0.0, col(C_LOW))
        act(q, ap("pb7", 1, 512, 2), ap("cc", 0, 256), col(C_16), col(C_LOW))
        m, k = 512 // cfg["cuts"], 0
        for x in range(0, 512, m):
            vec(q, "ts1", ap("bmt", x, x + m, 1, LO), ap("bmc", x, x + m, 1, LO), 5, A.logical_shift_right)
            vec(q, "ts1", ap("bmt", x, x + m, 1, HI), ap("bmc", x, x + m, 1, LO if cfg["once"] else HI), 31, A.bitwise_and)
            vec(q, "tt", ap("hl", x, x + m), ap("bmt", x, x + m), ap("pb7", x, x + m), A.add)
        for x in range(0, 512, m):
            for o in range(8):
                b, lo, c = ap("pb%d" % (k % 7 if m < 512 else 2 + o % 5), 0, m), 8 + 512 * o + x, -8192.0 * o - 65536.0 * q
                mm(q, b, ap("sm", 128 * o, 128 * o + 128), ap("hl", x, x + m), True, True)
                if cfg["evac"][q][k] == "a":
                    act(q, ap("yt", lo, lo + m), b, c)
                else:
                    built = vec(q, "ts1", ap("yt", lo, lo + m), b, c, A.add)
                k += 1
        for i in range(begin, built if q else 0):
            if ops[i]["e"] == "v" and ops[i]["name"] == "csi":
                late.append((i, built))
        for b in sorted({sum_at(q, P * h, P * h)[0] for h in range(q, NR)}):
            mm(q, ap(b, 0, 512), ap("zb", 0, 128), ap("lsb", 8, 520), True, False)
        if not CAST and floats(q):
            for x in range(0, 2048, 512):
                hi = x + 512 + (16 if x == 1536 else 0)
                vec(q, "ts1", ap("csf", x, hi), ap("csi", x, hi), -MID, A.add)

    def visitors_v(q):
        for h in range(NR - 1, q, -1):
            dma(q, "s", ap("vc", 4 * P * h, 4 * P * (h + 1), 1, EIGHT), ap("vd%d" % h, 0, 64), 2000)

    def zero_bin():
        at = ap("oz", 0, 1)
        vec(0, "ts2", at, ap("yt", 8, 9), 1.0 / 32, 8 + 16.5 / 32, A.mult, A.add)
        gather(0, "a", ap("zi", 0, 16), CSF, at)
        act(0, ap("csf", 0, 8), ap("zi", 0, 8))
        vec(0, "ts1", ap("csi", 0, 8), ap("zi", 0, 8), less(0), A.add)
        gather(0, "a", ap("zl", 0, 16), LS, at)
        act(0, ap("lsb", 0, 8), ap("zl", 0, 8))

    def chunks(lo, hi):
        return [(h, max(lo, P * h), min(hi, P * h + P)) for h in range((hi - 1) // P, lo // P - 1, -1)]

    def sum_at(q, lo, hi):
        h = lo // P
        b, x = ("pb0", 0) if h == q else ("pb1", P * (h - 2)) if h >= 2 else ("pb%d" % cfg["one"], P)
        return ap(b, x + lo - P * h, x + hi - P * h)

    def tally(q, lo, hi, src):
        i = mm(q, sum_at(q, lo, hi), ap("idn", 0, 128), src, False, False)
        ops[i]["sum"] = ops[i]["name"]

    back = {h: [] for h in range(NR)}

    def give_back(q, part, lo, hi):
        cut = chunks(lo, hi)
        least = min(len(topo.engines(cores[q], cores[x])) for x in range(q + 1, NR))
        same = [h for h, _, _ in cut if len(topo.engines(cores[q], cores[h])) > least]
        far = [x for x in range(q + 1, NR) if x not in same] if len(same) == len(cut) else []
        items = []
        for h, a, b in cut:
            x = P * (2 * q + part - h)
            src, dst = ("tw", "tf") if (h, part) in cfg["wide"][q] else ("tu", "tin")
            items.append((h, ap(src, 1024 * part + a, 1024 * part + b), ap(dst, x + a, x + b)))
            back[h].append((part, q, a - P * h, b - P * h))
        send(q, items, far if cfg["leave"] and part else ())

    def state(q, t, lo, hi):
        return wrapped("es", t, lo, hi) if q else last("dd", lo, hi)

    def report(q, src, dst, to):
        for run in (to[:cfg["apart"][q]], to[cfg["apart"][q]:]):
            if run:
                send(q, [(d, src, dst) for d in run])

    def task(q, t, lo, hi, ba, bb, on, lo2, hi2):
        n, own = hi - lo, lo // P == q
        if t == 1 and not own:
            vec(q, "ts1", state(q, 1, lo, hi), wrapped("land", 0, lo, hi), col(C_TOP), A.min)
        DD, XX, Y1, Y2 = ap("dd", lo, hi), ap("xx", lo, hi), ap("y1", lo, hi), ap("y2", lo, hi)
        E = state(q, t, lo, hi) if not own else last("y2", lo, hi) if t else last("dd", lo, hi)
        O1, O2 = wrapped("o1", t, lo, hi), wrapped("o2", t, lo, hi)
        vec(q, "ts2", O1, E, 1.0 / 16, col(C_K1), A.mult, A.add)
        if E[0] != "dd":
            (vec(q, "cp", last("dd", lo, hi), E) if on[3] == "v" else act(q, last("dd", lo, hi), E))
        gather(q, on[0], XX, ap("yt", 0, 4112), O1)
        vec(q, "scan", Y1, XX, DD)
        if q == 0 and lo >= 2 * P and t < 4 and cfg["load"] in ("v", "a"):
            (vec(q, "cp", ap("vb", lo, hi), XX) if cfg["load"] == "v" else act(q, ap("vb", lo, hi), XX))
        vec(q, "ts2", O2, last("y1", lo, hi), 1.0 / 32, col(C_K2), A.mult, A.add)
        cg, zc, CAST, LESS = "cg", 1024 * (t % 2), cfg["cast"][q], less(q)
        if t == 1 and lo // P in cfg["early"][q] and (lo // P, 0) in cfg["wide"][q]:
            cg, zc = "tw", 0
        fused = on[1] in "fF" and t < 4
        cs_on = "v" if t == 0 or on[1] in "vF" else "a"

        def sections(a, b):
            gather(q, cs_on, ap(cg, zc + a, zc + b), CSF if cs_on == "a" else CSI, wrapped("o2", t, a, b), -LESS)
        if t == 4 and not own:
            for h, a, b in chunks(lo, hi):
                if h in cfg["whole"][q]:
                    sections(a, b)
                    tally(q, a, b, ap("cg", zc + a, zc + b))
                else:
                    if h in cfg["pair"][q]:
                        vec(q, "tt", ap("tw", 1024 + a, 1024 + b), ind(CSF, wrapped("o2", t, a, b)), ap("cg", 1024 + a, 1024 + b), A.add)
                    elif (h, 1) in cfg["wide"][q]:
                        gather(q, "a", ap("tw", 1024 + a, 1024 + b), CSF, wrapped("o2", t, a, b))
                    else:
                        gather(q, "v", ap("tu", 1024 + a, 1024 + b), CSI, wrapped("o2", t, a, b))
                    give_back(q, 1, a, b)
            return
        if not fused:
            sections(lo, hi)
        if t < 4:
            LG, CM, YB = ap("lg", lo, hi), ap("cmpb", lo, hi), ap("yb", lo, hi)
            PA, PX = ap("pb%d" % ba, 0, n), ap("pb%d" % bb, P * (ba == bb), P * (ba == bb) + n)
            mm(q, PA, ap("g8h", 0, 128, 1, EIGHT), ap("vc", 4 * lo + t, 4 * hi, 4, EIGHT), True, fused or not CAST)
            for _ in range(cfg["again"] * (q == 0)):
                mm(q, PA, ap("g8h", 0, 128, 1, EIGHT), ap("vc", 4 * lo + t, 4 * hi, 4, EIGHT), True, True)
            if fused:
                act(q, ap("vb", lo, hi), PA, MID)
                vec(q, "tt", CM, ind(CSI, O2), ap("vb", lo, hi), A.is_gt)
            else:
                if CAST:
                    mm(q, PA, ap("mid", 0, 128, 1, (0, 1)), ap("onb", 0, n, 1, (0, 1)), False, True)
                vec(q, "tt", CM, ap(cg, zc + lo, zc + hi), PA, A.is_gt)
            gather(q, on[2], LG, LS, O2)
            mm(q, PX, ap("wk", 0, 128), CM, True, False)
            pick = mm(q, PX, ap("idb", 0, 128), LG, False, True)
            if ba != bb:
                ops[mm(q, PA, ap("wc", 0, 128), CM, True, False)]["deps"].add(pick)
            vec(q, "ts2", YB, PX, 0.0, CAP, A.max, A.min)
            if ba == bb:
                mm(q, PA, ap("wc", 0, 128), CM, True, False)
            pick = mm(q, PA, ap("wy", 0, 128), YB, False, True)
            vec(q, "scan", Y2, PA, DD)
            NEW, ES, LAND = last("y2", lo, hi), state(q, t + 1, lo, hi), wrapped("land", t, lo, hi)
            lower = list(range(q - 1, -1, -1))
            direct = cfg["direct"] and t == 1 and lo >= P * (NR - 1) and not own
            if own:
                if q > 0:
                    act(q, ES, NEW)
                    if lo2 < hi2:
                        report(q, state(q, t + 1, lo2, hi2), wrapped("land", t, lo2, hi2), lower if t == 0 else lower[:1])
            elif direct and q < NR - 2:
                mine = wrapped("mine", 0, lo, hi)
                if q > 0:
                    act(q, mine, NEW)
                    send(q, [(d, mine, wrapped("more", q, lo, hi)) for d in lower])
                for s in range(q + 1, NR - 2):
                    vec(q, "tt", mine, wrapped("more", s, lo, hi), NEW, A.min)
                    NEW = mine
                vec(q, "tt", ES, LAND, NEW, A.min)
            else:
                vec(q, "tt", ES, LAND, NEW, A.min)
                if q > 0:
                    report(q, ES, LAND, lower if direct else lower[:1])
            if fused:
                sections(lo, hi)
        for h, a, b in chunks(lo, hi):
            if t == 1 and h in cfg["early"][q]:
                if cg == "cg":
                    vec(q, "ts1", ap("tu", a, b), ap(cg, zc + a, zc + b), LESS, A.add)
                give_back(q, 0, a, b)
                continue
            if t == 3 and h in cfg["pair"][q]:
                continue
            tally(q, a, b, ap(cg, zc + a, zc + b))
            if t < 4:
                ops[-1]["deps"].add(pick)

    def sums(q, upto):
        hs = [h for h in range(q + 1, NR) if upto == (4 if h in cfg["whole"][q] else 2 if h in cfg["pair"][q] else 3)]
        for run in [[h] for h in hs[::-1]] if cfg["single"] else ([h for h in hs if h >= 2], [h for h in hs if h < 2]):
            if run:
                a, e = P * run[0], P * run[-1] + P
                b, x = sum_at(q, a, a)[:2]
                part = int(run[0] in cfg["early"][q])
                plus = (upto - part) * less(q)
                if (run[0], part) in cfg["wide"][q]:
                    act(q, ap("tw", 1024 * part + a, 1024 * part + e), ap(b, x, x + e - a), plus)
                else:
                    vec(q, "ts1", ap("tu", 1024 * part + a, 1024 * part + e), ap(b, x, x + e - a), plus, A.add)
                give_back(q, part, a, e)

    def finish(q):
        OWN, ACC = ap("pb0", 0, P), ap("acc", 0, P)

        def when(part, s):
            return -9 if q in cfg["early"][s] and not part else 1.5 * (part or q in cfg["whole"][s]) - s
        come = sorted({(when(part, s), part, s) for part, s, _, _ in back[q]})
        cut = max(0, len(come) - cfg["chain"][q])
        for _, part, s in come[:cut]:
            x = P * (2 * s + part)
            if (q, part) not in cfg["wide"][s]:
                vec(q, "cp", ap("tf", x, x + P), ap("tin", x, x + P))
            tally(q, P * q, P * q + P, ap("tf", x, x + P))
        act(q, ACC, OWN, col(C_END) if q else 5 * less(q))
        for k, (_, part, s) in enumerate(come[cut:]):
            x, pb = P * (2 * s + part), "pb%d" % (2 + k)
            for a, b in sorted(c[2:] for c in back[q] if c[:2] == (part, s)):
                vec(q, "cp", ap(pb, a, b), ap("tin", x + a, x + b))
                vec(q, "tt", ap("acc", P * k + P + a, P * k + P + b), ap("acc", P * k + a, P * k + b), ap(pb, a, b), A.add)
                if k == len(come) - cut - 1:
                    dma(q, "s", ap("y", a, b), ap("acc", P * k + P + a, P * k + P + b), 1500 + 2 * (b - a))
        if not come:
            dma(q, "s", ap("y", 0, P), ACC, 2000)

    for q in range(NR):
        start(q)
    for rnd in range(6):
        for q in range(NR - 1, -1, -1):
            if rnd >= 4:
                sums(q, rnd - 2)
            for k, s in reversed(list(enumerate(cfg["streams"][q]))):
                t = rnd if s[0] // P == q else rnd - 1
                if t <= 4 and (t > 0 or t == rnd):
                    cut = cfg["split"].get((q, t)) if s[0] // P == q else None
                    for x, piece in enumerate(cut or [s]):
                        tag[0] = "%d%d%d" % (q, rnd, k) + "abcd"[x] * bool(cut)
                        task(q, t, *piece, *((s[0], s[1]) if cut and x == len(cut) - 1 else (0, 0) if cut else piece[:2]))
                    tag[0] = None
            if rnd == 0:
                visitors_v(q)
                if q == 0:
                    zero_bin()
            if rnd == 5:
                sums(q, 4)
    for q in range(NR):
        finish(q)

    n = len(ops)
    users = [[] for _ in range(n)]
    for i, o in enumerate(ops):
        for j in o["deps"]:
            users[j].append(i)
    tail = [0.0] * n
    for i in range(n - 1, -1, -1):
        tail[i] = ops[i]["busy"] + ops[i]["lat"] + max([tail[u] + HOP for u in users[i]] + [0.0])
    for i, j in late:
        ops[i]["deps"].add(j)
        users[j].append(i)
    queue = [5 * o["q"] + "vapgs".index(o["e"]) for o in ops]
    gap = [[(u, 0.0 if queue[u] == queue[i] and o["e"] == "p" else (o["lats"][ops[u]["q"]] if o["rem"] else o["lat"]) + HOP)
            for u in users[i]] for i, o in enumerate(ops)]
    NEVER = 1e18

    def schedule(prio):
        rank = [tail[i] + prio.get(o["tag"], 0.0) + o.get("boost", 0.0) - 1e-3 * i for i, o in enumerate(ops)]
        left, can, at, end = [len(o["deps"]) for o in ops], [0.0] * n, [0.0] * n, 0.0
        ready, free, used = [[] for _ in range(5 * NR)], [0.0] * (5 * NR), [set() for _ in range(NR)]
        for i in range(n):
            if not left[i]:
                ready[queue[i]].append(i)
        soon = [0.0 if r else NEVER for r in ready]
        for _ in range(n):
            t, k = min((max(a, b), k) for k, (a, b) in enumerate(zip(soon, free)))
            i = max((i for i in ready[k] if can[i] <= t + cfg["look"][k // 5]), key=lambda i: rank[i])
            ready[k].remove(i)
            at[i] = max(t, can[i])
            e = at[i] + ops[i]["busy"]
            if ops[i]["rem"]:
                e += (0.0 if used[k // 5] else cfg["first"]) + cfg["fresh"] * len(ops[i]["uses"] - used[k // 5])
                used[k // 5] |= ops[i]["uses"]
            free[k] = e
            end = max(end, e + ops[i]["lat"])
            soon[k] = min([can[j] for j in ready[k]] + [NEVER])
            for u, d in gap[i]:
                can[u] = max(can[u], e + d)
                left[u] -= 1
                if not left[u]:
                    ready[queue[u]].append(u)
                    soon[queue[u]] = min(soon[queue[u]], can[u])
        return end, at

    tags, seed, prio = sorted({o["tag"] for o in ops if o["tag"]}), cfg["seed"], dict(cfg["prio"])
    now = best = schedule(prio)
    for step in range(cfg["tries"]):
        trial = dict(prio)
        for _ in range(2):
            seed = (seed * 1103515245 + 12345) % 2147483648
            tg = tags[(seed >> 8) % len(tags)]
            trial[tg] = trial.get(tg, 0.0) + (-3000, -1500, -500, 500, 1500, 3000)[(seed >> 20) % 6]
        res = schedule(trial)
        if res[0] <= now[0] + cfg["slack"] * (1 - step / cfg["tries"]):
            prio, now = trial, res
            best = min(best, res, key=lambda x: x[0])
    order = sorted(range(n), key=lambda i: (best[1][i], i))

    above, before = [0] * n, [[] for _ in range(n)]
    place = {i: k for k, i in enumerate(order)}
    for i in range(n):
        for u, d in gap[i]:
            before[u].append((i, d))
    for i in order:
        keep = []
        for j, d in sorted(before[i], key=lambda x: -place[x[0]]):
            if not above[i] >> j & 1 or ops[j]["lat"] > HOP:
                keep.append((j, d))
                above[i] |= above[j] | 1 << j
        before[i] = keep
    busy, lat, uses = [o["busy"] for o in ops], [o["lat"] for o in ops], [o.get("uses") for o in ops]

    def replay(order):
        fin, why, prev, free, used, end, top = [0.0] * n, [0] * n, [-1] * (5 * NR), [0.0] * (5 * NR), [set() for _ in range(5 * NR)], 0.0, 0
        rows = {}
        for i in order:
            k = queue[i]
            t, w = free[k], -2 - prev[k]
            for j, d in before[i]:
                if fin[j] + d > t:
                    t, w = fin[j] + d, j
            t += busy[i]
            if uses[i]:
                t += (0.0 if used[k] else cfg["first"]) + cfg["fresh"] * len(uses[i] - used[k])
                used[k] |= uses[i]
            free[k] = t
            if uses[i] and cfg["holds"]:
                t = max([t] + [rows.get((k, e), 0.0) for e in uses[i]])
                for e, d in ops[i]["hold"]:
                    rows[(k, e)] = t + d
            fin[i] = t
            prev[k], why[i] = i, w
            if t + lat[i] > end:
                end, top = t + lat[i], i
        return end, fin, why, top

    def price(w):
        bs, ls, tr = [], [], []
        for o in ops:
            picks = any(a[0] == "@" for a in o["args"] if isinstance(a, tuple))
            moves = []
            if o["rem"]:
                b, l = w["issue"], 0.0
                for core, mask, _, a, _ in o["args"][1]:
                    d = cores.index(core)
                    x, es = near(o["q"], d), [16 * o["q"] + e for e in range(16) if mask >> e & 1]
                    size = (a[2] - a[1]) * (4 if SCRATCH[a[0]][2] == F else 2)
                    moves.append((d, es, w["rem"][x], 128 / len(es) * (w["row"][x] + size * w["byte"][x])))
            elif o["sem"]:
                b, l = (w["dq"], w["t"].get(o["name"], w["t"]["in"])) if o["e"] != "g" else (o["busy"], o["lat"])
            elif o["e"] in "va":
                b, l = w["f" + o["e"]] + (o["busy"] - cfg["fix"] - 15 * (o["e"] == "a")) / CYC * w["cyc"] * (w["gat"] / GAT if picks else 1), 0.0
            elif o["e"] == "p":
                b, l = w["fp"] + (o["busy"] - cfg["pfix"]) / cfg["pe"] * w["pe"], w["lp"]
            else:
                b, l = o["busy"] * w["cyc"] / CYC, 0.0
            bs.append(b)
            ls.append(l)
            tr.append(moves)
        edges = [[(n + NR * j + o["q"], j, w["wake"]) if ops[j]["rem"] else
                  (j, j, ls[j] + w["hop"] if queue[j] != queue[i] or ops[j]["sem"] else 0.0 if o["e"] in "pg" else w["same"])
                  for j, _ in before[i]] for i, o in enumerate(ops)]
        return bs, ls, tr, edges, w["first"], w["fresh"]

    def walk(order, bs, ls, tr, edges, first, fresh):
        fin, why, prev, free, rows = [0.0] * (n * (NR + 1)), [0] * n, [-1] * (5 * NR), [0.0] * (5 * NR), [-1.0] * (16 * NR)
        end, top, called = 0.0, 0, [False] * (5 * NR)
        for i in order:
            k = queue[i]
            t, w = free[k], -2 - prev[k]
            for x, j, d in edges[i]:
                if fin[x] + d > t:
                    t, w = fin[x] + d, j
            t += bs[i]
            if tr[i]:
                t += (0.0 if called[k] else first) + fresh * sum(rows[e] < 0 for m in tr[i] for e in m[1])
                called[k] = True
                for d, es, start, span in tr[i]:
                    s = max([t + start] + [rows[e] for e in es]) + span
                    for e in es:
                        rows[e] = s
                    fin[n + NR * i + d] = s
            fin[i] = free[k] = t
            prev[k], why[i] = i, w
            if t + ls[i] > end:
                end, top = t + ls[i], i
        return end, fin, why, top

    if cfg["worlds"]:
        prices, turn = [price(w) for w in cfg["worlds"]], [0]
        busy = prices[0][0]

        def replay(order):
            runs = [walk(order, *p) for p in prices]
            turn[0] += 1
            return (sum(r[0] for r in runs) / len(runs), runs[0][1]) + runs[turn[0] % len(runs)][2:]

    def swap(order, u, v):
        a, b = order.index(u), order.index(v)
        front, behind, moved, held = [], [], 0, set()
        for x in order[a:b]:
            if x == u or above[x] & moved or queue[x] in held:
                behind.append(x)
                moved |= 1 << x
                held.add(queue[x])
            else:
                front.append(x)
        return None if above[v] & moved else order[:a] + front + [v] + behind + order[b + 1:]

    now = best = (replay(order), order)
    barred = {}
    for step in range(cfg["swaps"]):
        pairs, i = [], now[0][3]
        while now[0][2][i] != -1:
            w = now[0][2][i]
            if w < -1:
                w = -2 - w
                if not above[i] >> w & 1 and "boost" not in ops[w]:
                    seed = (seed * 1103515245 + 12345) % 2147483648
                    pairs.append((seed >> 8, w, i))
            i = w
        found = None
        for _, u, v in sorted(pairs)[:12]:
            new = swap(now[1], u, v)
            res = new and replay(new)
            if res and (barred.get((v, u), -1) < step or res[0] < best[0][0]) and (not found or res[0] < found[0][0]):
                found = (res, new, u, v)
                if res[0] < now[0][0] - 1:
                    break
        if found:
            barred[found[2:]] = step + 8 + seed % 8
            now = found[:2]
            best = min(best, now, key=lambda x: x[0][0])
        else:
            now, barred = best, {}
    (end, fin, _, _), order = best
    for i, o in enumerate(ops):
        o["t"] = fin[i] - busy[i]
    count, closing = {}, {}
    for i in order:
        o = ops[i]
        if "sum" in o:
            closing[(o["q"], o["sum"])] = i
        if o["sem"]:
            o["sig"] = o["sem"]
        elif not o["rem"]:
            key = (o["q"], o["e"])
            count[key] = count.get(key, 0) + 1
            o["sig"] = (COUNT[o["e"]], count[key])
    for i in closing.values():
        ops[i]["args"][4] = True
    return ops, order, end


def emit(g, T, o, topo):
    if o["kind"] != "send":
        return CALLS[o["kind"]](g, *[real(T, a) for a in o["args"]])
    src, tr = o["args"][0], []
    for core, mask, sem, a, b in o["args"][1]:
        rid, pid = topo.addr(core, src)
        tr.append(RemoteDMATransfer(dst_ids=[DstId(rid=rid, pnc=pid)], dma_engine_mask=mask, remote_sem=T.sem[sem], src=real(T, a), dst=real(T, b)))
    return g.remote_dma_fused(tr, local_sem=T.sem.sent)


PLAN = {}


def rank_program(g, core, T, topo):
    q = T.rank_of(core)
    if q is None:
        return
    if "p" not in PLAN:
        PLAN["p"] = build(list(T.cores), topo, CFG)
    ops, order, _ = PLAN["p"]
    queue = {"g": g, "v": g.vector, "a": g.scalar, "p": g.tensor, "s": g.sync}
    seen, total, knew, waited, place = {}, {}, {}, set(), {i: k for k, i in enumerate(order)}
    for i in order:
        o = ops[i]
        if o["rem"] and q in o["rem"]:
            total[o["rem"][q][0]] = o["rem"][q][1]
        if o["q"] != q:
            continue
        know = seen.setdefault(o["e"], {})
        for j in sorted(o["deps"], key=lambda j: -place[j]):
            d = ops[j]
            if d["e"] == o["e"] and (d["e"] == "p" or d["e"] == "g" and not d["rem"] and (o["rem"] or d["args"][0] not in o["args"])):
                continue
            s, v = d["rem"][q] if d["rem"] else d["sig"]
            if know.get(s, 0) < v:
                queue[o["e"]].wait_ge(T.sem[s], v)
                waited.add((o["e"], s, v))
                know[s] = v
                for s2, v2 in knew.get(j, {}).items():
                    know[s2] = max(know.get(s2, 0), v2)
        knew[i] = dict(know)
        r = emit(g, T, o, topo)
        if o["rem"]:
            total["sent"] = total.get("sent", 0) + sum(v for _, v in o["rem"].values())
        else:
            r.then_inc(T.sem[o["sig"][0]], 16 if o["sem"] else 1)
            total[o["sig"][0]] = o["sig"][1]
    for s, v in total.items():
        if ("g", s, v) not in waited:
            g.wait_ge(T.sem[s], v)
